import numpy as np
import ml_dtypes


def mxq(x, axis, fmt="e4m3"):
    dtype, down = {"e4m3": (ml_dtypes.float8_e4m3fn, 7), "e5m2": (ml_dtypes.float8_e5m2, 14)}[fmt]
    v = np.moveaxis(np.asarray(x, np.float32).astype(ml_dtypes.bfloat16).astype(np.float64), axis, -1)
    blocks = v.reshape(v.shape[:-1] + (-1, 32))
    amax = np.abs(blocks).max(-1, keepdims=True)
    byte = np.maximum(np.where(amax > 0, np.frexp(amax)[1] - 1 + 127, 0) - down, 1)
    scale = np.exp2(byte - 127.0)
    codes = (blocks / scale).astype(np.float32).astype(dtype).astype(np.float64)
    return np.moveaxis((codes * scale).reshape(v.shape), -1, axis)


WIDE = False


def mx_kscale(k):
    if not WIDE:
        return np.ones(k)
    levels = np.array([10, -10, 5, -5, 0])
    if k % 512:
        return np.exp2(np.random.permutation(np.resize(levels, k // 32))).repeat(32)
    a = np.empty((k // 512, 16))
    for p in range(k // 512):
        a[p, :8] = np.random.permutation(np.resize(levels, 8))
        for g in range(8):
            far = levels[np.abs(levels - a[p, g]) >= 10]
            a[p, g + 8] = far[np.random.randint(len(far))]
    return np.exp2(a.ravel()).repeat(32)


def f64(x):
    return np.asarray(x).astype(np.float64)


def striped(idx):
    return np.tile(idx.reshape(-1, 16).T, (8, 1)).astype(np.uint16)


def unstriped(offs):
    return offs[:16].T.reshape(-1).astype(np.int64)


E2M1 = np.array([0.0, 0.5, 1.0, 1.5, 2.0, 3.0, 4.0, 6.0, -0.0, -0.5, -1.0, -1.5, -2.0, -3.0, -4.0, -6.0])


def pack_fp4(w):
    k, n = w.shape
    w = f64(np.asarray(w, np.float32).astype(ml_dtypes.bfloat16)).reshape(k // 32, 32, n)
    amax = np.abs(w).max(1)
    mant, ex = np.frexp(amax / 6.0)
    byte = np.clip(np.where(amax > 0, np.where(mant > 0.5, ex, ex - 1) + 127, 1), 1, 254)
    scaled = (w * np.exp2(127.0 - byte)[:, None, :]).reshape(k, n).astype(np.float32)
    c = np.ascontiguousarray(scaled.reshape(k // 512, 128, 4, n).transpose(0, 1, 3, 2)).astype(ml_dtypes.float4_e2m1fn).view(np.uint8) & 0xF
    words = (c[..., 0::2] | (c[..., 1::2] << 4)).reshape(k // 512, 128, 2 * n)
    return np.ascontiguousarray(words), np.ascontiguousarray(byte.astype(np.uint8).reshape(k // 512, 16, n))


def unpack_fp4(words, scales):
    g, _, n = scales.shape
    words = np.ascontiguousarray(words).reshape(g, 128, n, 2)
    nib = np.empty((g, 128, n, 4), np.uint8)
    nib[..., 0::2] = words & 0xF
    nib[..., 1::2] = words >> 4
    vals = E2M1[nib] * np.repeat(np.exp2(scales.astype(np.float64) - 127.0), 8, axis=1)[..., None]
    return vals.transpose(0, 1, 3, 2).reshape(g * 512, n)


def relu(v):
    return np.maximum(v, 0.0)


K, T, S, N, U = 1024, 2048, 1024, 256, 2048


def setup_inputs():
    n = np.random.standard_normal
    s = mx_kscale(K)[:, None]
    packed_w1 = pack_fp4(n((K, N)) / np.sqrt(K) / s)
    return {
        "xT": (n((K, T)) * s).astype(np.float32),
        "w1_words": packed_w1[0],
        "w1_scales": packed_w1[1],
        "res": n((N, U)).astype(np.float32),
        "offs": striped(np.random.permutation(T)[:S]),
        "own": striped(np.random.randint(0, S, U)),
    }


def reference(xT, w1_words, w1_scales, res, offs, own):
    xq = mxq(f64(xT)[:, unstriped(offs)], 0, "e4m3")
    y = relu(unpack_fp4(w1_words, w1_scales).T @ xq)
    return f64(res) + y[:, unstriped(own)]

@@ -1,0 +1,150 @@
+from contextlib import ExitStack
+
+import concourse.mybir as mybir
+
+K, T, S, N, U = 1024, 2048, 1024, 256, 2048
+FLOPS = 2 * K * S * N
+
+F32 = mybir.dt.float32
+BF16 = mybir.dt.bfloat16
+I32 = mybir.dt.int32
+U32 = mybir.dt.uint32
+U16 = mybir.dt.uint16
+U8 = mybir.dt.uint8
+FP8X4 = mybir.dt.float8_e4m3fn_x4
+FP4X4 = mybir.dt.float4_e2m1fn_x4
+ACT = mybir.ActivationFunctionType
+ADD = mybir.AluOpType.add
+
+P = 128
+PASSES = 2
+BLOCKS = 2
+PIECE = 256
+HALF = 512
+SMALL = 128
+
+LOADS = [
+    [(0, 2048, 1280)],
+    [(0, 1024, 0), (1024, 1024, 672)],
+    [(0, 1024, 0), (1024, 1024, 256)],
+    [(0, 1024, 0), (1024, 512, 512), (1536, 512, 256)],
+]
+OUT_PIECES = [[768, 768, 512], [768, 640, 384, 256]]
+
+
+def tile_picked_unmerge_relu_e_kernel(tc, xT, w1_words, w1_scales, res, offs, own, out):
+    nc = tc.nc
+    with ExitStack() as ctx:
+        keep = ctx.enter_context(tc.tile_pool(name="keep", bufs=1))
+        psum = ctx.enter_context(tc.psum_pool(name="psum", bufs=1))
+
+        offs_sb = keep.tile([P, S // 16], U16, name="offs_sb")
+        own_sb = keep.tile([P, U // 16], U16, name="own_sb")
+        w_words = keep.tile([P, PASSES, 2 * N], U8, name="w_words", align_bytes=64)
+        w_scales = keep.tile([P, PASSES, N], U8, name="w_scales", align_bytes=64)
+        nc.gpsimd.memset(w_scales[:].bitcast(I32), 0)
+
+        x_rows = xT.rearrange("(z p u j) t -> z u p j t", z=PASSES, p=P, u=2, j=2)
+        raw = {}
+        for q in range(4):
+            for (t0, width, vshare) in LOADS[q]:
+                raw[q, t0] = keep.tile([P, 2, width], F32, name="raw_%d_%d" % (q, t0))
+                nc.sync.dma_start(raw[q, t0][:], x_rows[q // 2, q % 2][:, :, t0 : t0 + width])
+                if q == 0 and t0 == 0:
+                    nc.sync.dma_start(offs_sb[:], offs)
+        nc.sync.dma_start(w_words[:].bitcast(I32), w1_words.rearrange("z p c -> p z c").bitcast(I32))
+        for quad in range(4):
+            nc.sync.dma_start(
+                w_scales[32 * quad : 32 * quad + 4, :, :].bitcast(I32),
+                w1_scales[:, 4 * quad : 4 * quad + 4, :].rearrange("z r c -> r z c").bitcast(I32),
+            )
+        nc.sync.dma_start(own_sb[:], own)
+        res_sb = []
+        for b in range(BLOCKS):
+            res_sb.append(keep.tile([P, U], F32, name="res_%d" % b))
+            nc.sync.dma_start(res_sb[b][:], res[b * P : (b + 1) * P, :])
+
+        pairs = [keep.tile([P, 2 * T], BF16, name="pairs_%d" % q) for q in range(4)]
+        picked = [keep.tile([P, 4 * S], BF16, name="picked_%d" % z) for z in range(PASSES)]
+        woven = [keep.tile([P, 4 * S], BF16, name="woven_%d" % z, align_bytes=64) for z in range(PASSES)]
+        codes = [keep.tile([P, S], U32, name="codes_%d" % z, align_bytes=64) for z in range(PASSES)]
+        scales = [keep.tile([P, S], U8, name="scales_%d" % z, align_bytes=64) for z in range(PASSES)]
+
+        def cast(q):
+            for (t0, width, on_vector) in LOADS[q]:
+                src = raw[q, t0][:].rearrange("p j t -> p t j")
+                dst = pairs[q][:, 2 * t0 : 2 * (t0 + width)].rearrange("p (t j) -> p t j", j=2)
+                on_scalar = width - on_vector
+                if on_vector:
+                    nc.vector.tensor_copy(dst[:, on_scalar:, :], src[:, on_scalar:, :])
+                if on_scalar:
+                    nc.scalar.activation(dst[:, :on_scalar, :], src[:, :on_scalar, :], ACT.Copy)
+
+        def gather(q, e0, n):
+            dst = picked[q // 2][:].bitcast(U32)[:, (q % 2) * S + e0 : (q % 2) * S + e0 + n]
+            nc.vector.tensor_copy(dst, pairs[q][:].bitcast(U32).indirect(offs_sb[:, e0 // 16 : (e0 + n) // 16]))
+
+        def weave_views(z, e0, n, dt):
+            src = picked[z][:].bitcast(dt).rearrange("p (u e) -> p e u", u=2)[:, e0 : e0 + n, :]
+            dst = woven[z][:].bitcast(dt)[:, 2 * e0 : 2 * (e0 + n)].rearrange("p (e u) -> p e u", u=2)
+            return dst, src
+
+        def quantize(z, e0, n):
+            nc.vector.quantize_mx(
+                out=codes[z][:, e0 : e0 + n].bitcast(FP8X4),
+                scales=scales[z][:, e0 : e0 + n],
+                in_=woven[z][:, 4 * e0 : 4 * (e0 + n)],
+            )
+
+        groups = [(0, 0, HALF), (1, 0, HALF)] + [(0, e0, SMALL) for e0 in range(HALF, S, SMALL)] + [(1, HALF, HALF)]
+        acc = [psum.tile([P, HALF], F32, name="acc_%d" % g) for g in range(len(groups))]
+        y = [keep.tile([P, S], F32, name="y_%d" % b) for b in range(BLOCKS)]
+
+        def multiply(g, z):
+            b, e0, n = groups[g]
+            nc.tensor.matmul_mx(
+                out=acc[g][:, :n],
+                lhsT=w_words[:, z, 2 * P * b : 2 * P * (b + 1)].bitcast(FP4X4),
+                lhsT_scale=w_scales[:, z, P * b : P * (b + 1)],
+                rhs=codes[z][:, e0 : e0 + n].bitcast(FP8X4),
+                rhs_scale=scales[z][:, e0 : e0 + n],
+                start=(z == 0),
+                stop=(z == PASSES - 1),
+            )
+
+        cast(0)
+        gather(0, 0, S)
+        cast(1)
+        gather(1, 0, S)
+        dst, src = weave_views(0, 0, S, I32)
+        nc.vector.tensor_copy(dst, src)
+        cast(2)
+        quantize(0, 0, S)
+        for g in range(len(groups)):
+            multiply(g, 0)
+        gather(2, 0, S)
+        cast(3)
+        for e0 in range(0, S, PIECE):
+            gather(3, e0, PIECE)
+            dst, src = weave_views(1, e0, PIECE, U32)
+            nc.scalar.copy(dst, src)
+        for e0 in range(0, S, PIECE):
+            quantize(1, e0, PIECE)
+        for g in [0, 2, 3, 4, 5, 1, 6]:
+            multiply(g, 1)
+        for g in [0, 2, 3, 4, 5, 1, 6]:
+            b, e0, n = groups[g]
+            if g in (2, 3, 4):
+                nc.vector.tensor_scalar_max(y[b][:, e0 : e0 + n], acc[g][:, :n], 0.0)
+            else:
+                nc.scalar.activation(y[b][:, e0 : e0 + n], acc[g][:, :n], ACT.Relu)
+
+        for b in range(BLOCKS):
+            r0 = 0
+            for n in OUT_PIECES[b]:
+                summed = keep.tile([P, n], F32, name="summed_%d_%d" % (b, r0))
+                nc.vector.tensor_tensor(
+                    summed[:], y[b][:].indirect(own_sb[:, r0 // 16 : (r0 + n) // 16]), res_sb[b][:, r0 : r0 + n], ADD
+                )
+                nc.sync.dma_start(out[b * P : (b + 1) * P, r0 : r0 + n], summed[:])
+                r0 = r0 + n

@@ -24,10 +24,10 @@ HALF = 512
 SMALL = 128
 
 LOADS = [
-    [(0, 2048, 1280)],
-    [(0, 1024, 0), (1024, 1024, 672)],
-    [(0, 1024, 0), (1024, 1024, 256)],
-    [(0, 1024, 0), (1024, 512, 512), (1536, 512, 256)],
+    [(0, 1024, 0), (1024, 1024, 640)],
+    [(0, 1024, 0), (1024, 1024, 640)],
+    [(0, 1024, 0), (1024, 1024, 640)],
+    [(0, 512, 0), (512, 512, 0), (1024, 512, 0), (1536, 512, 320)],
 ]
 OUT_PIECES = [[768, 768, 512], [768, 640, 384, 256]]
 
@@ -50,14 +50,14 @@ def tile_picked_unmerge_relu_e_kernel(tc, xT, w1_words, w1_scales, res, offs, ow
             for (t0, width, vshare) in LOADS[q]:
                 raw[q, t0] = keep.tile([P, 2, width], F32, name="raw_%d_%d" % (q, t0))
                 nc.sync.dma_start(raw[q, t0][:], x_rows[q // 2, q % 2][:, :, t0 : t0 + width])
-                if q == 0 and t0 == 0:
+                if q == 0 and t0 > 0:
                     nc.sync.dma_start(offs_sb[:], offs)
-        nc.sync.dma_start(w_words[:].bitcast(I32), w1_words.rearrange("z p c -> p z c").bitcast(I32))
         for quad in range(4):
             nc.sync.dma_start(
                 w_scales[32 * quad : 32 * quad + 4, :, :].bitcast(I32),
                 w1_scales[:, 4 * quad : 4 * quad + 4, :].rearrange("z r c -> r z c").bitcast(I32),
             )
+        nc.sync.dma_start(w_words[:].bitcast(I32), w1_words.rearrange("z p c -> p z c").bitcast(I32))
         nc.sync.dma_start(own_sb[:], own)
         res_sb = []
         for b in range(BLOCKS):
@@ -65,7 +65,7 @@ def tile_picked_unmerge_relu_e_kernel(tc, xT, w1_words, w1_scales, res, offs, ow
             nc.sync.dma_start(res_sb[b][:], res[b * P : (b + 1) * P, :])
 
         pairs = [keep.tile([P, 2 * T], BF16, name="pairs_%d" % q) for q in range(4)]
-        picked = [keep.tile([P, 4 * S], BF16, name="picked_%d" % z) for z in range(PASSES)]
+        picked = keep.tile([P, 4 * S], BF16, name="picked")
         woven = [keep.tile([P, 4 * S], BF16, name="woven_%d" % z, align_bytes=64) for z in range(PASSES)]
         codes = [keep.tile([P, S], U32, name="codes_%d" % z, align_bytes=64) for z in range(PASSES)]
         scales = [keep.tile([P, S], U8, name="scales_%d" % z, align_bytes=64) for z in range(PASSES)]
@@ -81,11 +81,15 @@ def tile_picked_unmerge_relu_e_kernel(tc, xT, w1_words, w1_scales, res, offs, ow
                     nc.scalar.activation(dst[:, :on_scalar, :], src[:, :on_scalar, :], ACT.Copy)
 
         def gather(q, e0, n):
-            dst = picked[q // 2][:].bitcast(U32)[:, (q % 2) * S + e0 : (q % 2) * S + e0 + n]
+            dst = picked[:].bitcast(U32)[:, (q % 2) * S + e0 : (q % 2) * S + e0 + n]
             nc.vector.tensor_copy(dst, pairs[q][:].bitcast(U32).indirect(offs_sb[:, e0 // 16 : (e0 + n) // 16]))
 
+        def gather_woven(q):
+            dst = woven[0][:].bitcast(U32).rearrange("p (e u) -> p e u", u=2)[:, :, q]
+            nc.vector.tensor_copy(dst, pairs[q][:].bitcast(U32).indirect(offs_sb[:]))
+
         def weave_views(z, e0, n, dt):
-            src = picked[z][:].bitcast(dt).rearrange("p (u e) -> p e u", u=2)[:, e0 : e0 + n, :]
+            src = picked[:].bitcast(dt).rearrange("p (u e) -> p e u", u=2)[:, e0 : e0 + n, :]
             dst = woven[z][:].bitcast(dt)[:, 2 * e0 : 2 * (e0 + n)].rearrange("p (e u) -> p e u", u=2)
             return dst, src
 
@@ -96,14 +100,12 @@ def tile_picked_unmerge_relu_e_kernel(tc, xT, w1_words, w1_scales, res, offs, ow
                 in_=woven[z][:, 4 * e0 : 4 * (e0 + n)],
             )
 
-        groups = [(0, 0, HALF), (1, 0, HALF)] + [(0, e0, SMALL) for e0 in range(HALF, S, SMALL)] + [(1, HALF, HALF)]
-        acc = [psum.tile([P, HALF], F32, name="acc_%d" % g) for g in range(len(groups))]
+        banks = [psum.tile([P, HALF], F32, name="bank_%d" % g) for g in range(8)]
         y = [keep.tile([P, S], F32, name="y_%d" % b) for b in range(BLOCKS)]
 
-        def multiply(g, z):
-            b, e0, n = groups[g]
+        def multiply(bank, b, e0, n, z):
             nc.tensor.matmul_mx(
-                out=acc[g][:, :n],
+                out=banks[bank][:, :n],
                 lhsT=w_words[:, z, 2 * P * b : 2 * P * (b + 1)].bitcast(FP4X4),
                 lhsT_scale=w_scales[:, z, P * b : P * (b + 1)],
                 rhs=codes[z][:, e0 : e0 + n].bitcast(FP8X4),
@@ -112,32 +114,42 @@ def tile_picked_unmerge_relu_e_kernel(tc, xT, w1_words, w1_scales, res, offs, ow
                 stop=(z == PASSES - 1),
             )
 
+        def weave(z, e0, n):
+            dst, src = weave_views(z, e0, n, U32)
+            nc.scalar.copy(dst, src)
+
         cast(0)
-        gather(0, 0, S)
+        gather_woven(0)
         cast(1)
-        gather(1, 0, S)
-        dst, src = weave_views(0, 0, S, I32)
-        nc.vector.tensor_copy(dst, src)
+        gather_woven(1)
         cast(2)
-        quantize(0, 0, S)
-        for g in range(len(groups)):
-            multiply(g, 0)
         gather(2, 0, S)
+        quantize(0, 0, S)
+        for g in range(8):
+            multiply(g, 0, g * SMALL, SMALL, 0)
         cast(3)
         for e0 in range(0, S, PIECE):
             gather(3, e0, PIECE)
-            dst, src = weave_views(1, e0, PIECE, U32)
-            nc.scalar.copy(dst, src)
-        for e0 in range(0, S, PIECE):
-            quantize(1, e0, PIECE)
-        for g in [0, 2, 3, 4, 5, 1, 6]:
-            multiply(g, 1)
-        for g in [0, 2, 3, 4, 5, 1, 6]:
-            b, e0, n = groups[g]
-            if g in (2, 3, 4):
-                nc.vector.tensor_scalar_max(y[b][:, e0 : e0 + n], acc[g][:, :n], 0.0)
+            if e0 + PIECE < S:
+                weave(1, e0, PIECE)
             else:
-                nc.scalar.activation(y[b][:, e0 : e0 + n], acc[g][:, :n], ACT.Relu)
+                weave(1, e0, SMALL)
+                weave(1, e0 + SMALL, SMALL)
+        for e0 in range(0, S - PIECE, PIECE):
+            quantize(1, e0, PIECE)
+        quantize(1, S - PIECE, SMALL)
+        quantize(1, S - SMALL, SMALL)
+        for g in range(8):
+            multiply(g, 0, g * SMALL, SMALL, 1)
+        for g in range(8):
+            if g == 7:
+                nc.vector.tensor_scalar_max(y[0][:, g * SMALL : (g + 1) * SMALL], banks[g][:, :SMALL], 0.0)
+            else:
+                nc.scalar.activation(y[0][:, g * SMALL : (g + 1) * SMALL], banks[g][:, :SMALL], ACT.Relu)
+        for h in range(2):
+            for z in range(PASSES):
+                multiply(6 + h, 1, h * HALF, HALF, z)
+            nc.scalar.activation(y[1][:, h * HALF : (h + 1) * HALF], banks[6 + h][:], ACT.Relu)
 
         for b in range(BLOCKS):
             r0 = 0

@@ -26,10 +26,10 @@ SMALL = 128
 LOADS = [
     [(0, 1024, 0), (1024, 1024, 640)],
     [(0, 1024, 0), (1024, 1024, 640)],
-    [(0, 1024, 0), (1024, 1024, 640)],
-    [(0, 512, 0), (512, 512, 0), (1024, 512, 0), (1536, 512, 320)],
+    [(0, 1024, 0), (1024, 1024, 320)],
+    [(0, 768, 0), (768, 768, 256), (1536, 512, 320)],
 ]
-OUT_PIECES = [[768, 768, 512], [768, 640, 384, 256]]
+OUT_PIECES = [[768, 768, 512], [768, 640, 288, 224, 128]]
 
 
 def tile_picked_unmerge_relu_e_kernel(tc, xT, w1_words, w1_scales, res, offs, own, out):
@@ -48,7 +48,7 @@ def tile_picked_unmerge_relu_e_kernel(tc, xT, w1_words, w1_scales, res, offs, ow
         raw = {}
         for q in range(4):
             for (t0, width, vshare) in LOADS[q]:
-                raw[q, t0] = keep.tile([P, 2, width], F32, name="raw_%d_%d" % (q, t0))
+                raw[q, t0] = keep.tile([P, 2, width], F32, name="raw_%d_%d" % (q, t0), tag="raw_%d_%d" % (q, t0))
                 nc.sync.dma_start(raw[q, t0][:], x_rows[q // 2, q % 2][:, :, t0 : t0 + width])
                 if q == 0 and t0 > 0:
                     nc.sync.dma_start(offs_sb[:], offs)
@@ -59,12 +59,8 @@ def tile_picked_unmerge_relu_e_kernel(tc, xT, w1_words, w1_scales, res, offs, ow
             )
         nc.sync.dma_start(w_words[:].bitcast(I32), w1_words.rearrange("z p c -> p z c").bitcast(I32))
         nc.sync.dma_start(own_sb[:], own)
-        res_sb = []
-        for b in range(BLOCKS):
-            res_sb.append(keep.tile([P, U], F32, name="res_%d" % b))
-            nc.sync.dma_start(res_sb[b][:], res[b * P : (b + 1) * P, :])
 
-        pairs = [keep.tile([P, 2 * T], BF16, name="pairs_%d" % q) for q in range(4)]
+        pairs = [keep.tile([P, 2 * T], BF16, name="pairs_%d" % q, tag="pairs_%d" % q) for q in range(4)]
         picked = keep.tile([P, 4 * S], BF16, name="picked")
         woven = [keep.tile([P, 4 * S], BF16, name="woven_%d" % z, align_bytes=64) for z in range(PASSES)]
         codes = [keep.tile([P, S], U32, name="codes_%d" % z, align_bytes=64) for z in range(PASSES)]
@@ -76,7 +72,10 @@ def tile_picked_unmerge_relu_e_kernel(tc, xT, w1_words, w1_scales, res, offs, ow
                 dst = pairs[q][:, 2 * t0 : 2 * (t0 + width)].rearrange("p (t j) -> p t j", j=2)
                 on_scalar = width - on_vector
                 if on_vector:
-                    nc.vector.tensor_copy(dst[:, on_scalar:, :], src[:, on_scalar:, :])
+                    nc.vector.tensor_copy(
+                        dst[:, on_scalar:, :].rearrange("p (c i) j -> p c j i", i=4),
+                        src[:, on_scalar:, :].rearrange("p (c i) j -> p c j i", i=4),
+                    )
                 if on_scalar:
                     nc.scalar.activation(dst[:, :on_scalar, :], src[:, :on_scalar, :], ACT.Copy)
 
@@ -122,9 +121,9 @@ def tile_picked_unmerge_relu_e_kernel(tc, xT, w1_words, w1_scales, res, offs, ow
         gather_woven(0)
         cast(1)
         gather_woven(1)
+        quantize(0, 0, S)
         cast(2)
         gather(2, 0, S)
-        quantize(0, 0, S)
         for g in range(8):
             multiply(g, 0, g * SMALL, SMALL, 0)
         cast(3)
@@ -135,6 +134,10 @@ def tile_picked_unmerge_relu_e_kernel(tc, xT, w1_words, w1_scales, res, offs, ow
             else:
                 weave(1, e0, SMALL)
                 weave(1, e0 + SMALL, SMALL)
+        res_sb = []
+        for b, tag in enumerate(["raw_3_%d" % LOADS[3][-1][0], "pairs_3"]):
+            res_sb.append(keep.tile([P, U], F32, name="res_%d" % b, tag=tag))
+            nc.sync.dma_start(res_sb[b][:], res[b * P : (b + 1) * P, :])
         for e0 in range(0, S - PIECE, PIECE):
             quantize(1, e0, PIECE)
         quantize(1, S - PIECE, SMALL)

@@ -24,9 +24,9 @@ HALF = 512
 SMALL = 128
 
 LOADS = [
+    [(0, 2048, 1280)],
     [(0, 1024, 0), (1024, 1024, 640)],
-    [(0, 1024, 0), (1024, 1024, 640)],
-    [(0, 1024, 0), (1024, 1024, 320)],
+    [(0, 2048, 1280)],
     [(0, 768, 0), (768, 768, 256), (1536, 512, 320)],
 ]
 OUT_PIECES = [[768, 768, 512], [768, 640, 288, 224, 128]]
@@ -50,7 +50,7 @@ def tile_picked_unmerge_relu_e_kernel(tc, xT, w1_words, w1_scales, res, offs, ow
             for (t0, width, vshare) in LOADS[q]:
                 raw[q, t0] = keep.tile([P, 2, width], F32, name="raw_%d_%d" % (q, t0), tag="raw_%d_%d" % (q, t0))
                 nc.sync.dma_start(raw[q, t0][:], x_rows[q // 2, q % 2][:, :, t0 : t0 + width])
-                if q == 0 and t0 > 0:
+                if q == 0:
                     nc.sync.dma_start(offs_sb[:], offs)
         for quad in range(4):
             nc.sync.dma_start(
@@ -61,7 +61,7 @@ def tile_picked_unmerge_relu_e_kernel(tc, xT, w1_words, w1_scales, res, offs, ow
         nc.sync.dma_start(own_sb[:], own)
 
         pairs = [keep.tile([P, 2 * T], BF16, name="pairs_%d" % q, tag="pairs_%d" % q) for q in range(4)]
-        picked = keep.tile([P, 4 * S], BF16, name="picked")
+        picked = [keep.tile([P, 4 * S], BF16, name="picked_%d" % z) for z in range(PASSES)]
         woven = [keep.tile([P, 4 * S], BF16, name="woven_%d" % z, align_bytes=64) for z in range(PASSES)]
         codes = [keep.tile([P, S], U32, name="codes_%d" % z, align_bytes=64) for z in range(PASSES)]
         scales = [keep.tile([P, S], U8, name="scales_%d" % z, align_bytes=64) for z in range(PASSES)]
@@ -80,15 +80,11 @@ def tile_picked_unmerge_relu_e_kernel(tc, xT, w1_words, w1_scales, res, offs, ow
                     nc.scalar.activation(dst[:, :on_scalar, :], src[:, :on_scalar, :], ACT.Copy)
 
         def gather(q, e0, n):
-            dst = picked[:].bitcast(U32)[:, (q % 2) * S + e0 : (q % 2) * S + e0 + n]
+            dst = picked[q // 2][:].bitcast(U32)[:, (q % 2) * S + e0 : (q % 2) * S + e0 + n]
             nc.vector.tensor_copy(dst, pairs[q][:].bitcast(U32).indirect(offs_sb[:, e0 // 16 : (e0 + n) // 16]))
 
-        def gather_woven(q):
-            dst = woven[0][:].bitcast(U32).rearrange("p (e u) -> p e u", u=2)[:, :, q]
-            nc.vector.tensor_copy(dst, pairs[q][:].bitcast(U32).indirect(offs_sb[:]))
-
         def weave_views(z, e0, n, dt):
-            src = picked[:].bitcast(dt).rearrange("p (u e) -> p e u", u=2)[:, e0 : e0 + n, :]
+            src = picked[z][:].bitcast(dt).rearrange("p (u e) -> p e u", u=2)[:, e0 : e0 + n, :]
             dst = woven[z][:].bitcast(dt)[:, 2 * e0 : 2 * (e0 + n)].rearrange("p (e u) -> p e u", u=2)
             return dst, src
 
@@ -118,10 +114,13 @@ def tile_picked_unmerge_relu_e_kernel(tc, xT, w1_words, w1_scales, res, offs, ow
             nc.scalar.copy(dst, src)
 
         cast(0)
-        gather_woven(0)
+        gather(0, 0, S)
         cast(1)
-        gather_woven(1)
-        quantize(0, 0, S)
+        for e0 in range(0, S, PIECE):
+            gather(1, e0, PIECE)
+            weave(0, e0, PIECE)
+        for e0 in range(0, S, HALF):
+            quantize(0, e0, HALF)
         cast(2)
         gather(2, 0, S)
         for g in range(8):

@@ -26,10 +26,10 @@ SMALL = 128
 LOADS = [
     [(0, 2048, 1280)],
     [(0, 1024, 0), (1024, 1024, 640)],
-    [(0, 2048, 1280)],
-    [(0, 768, 0), (768, 768, 256), (1536, 512, 320)],
+    [(0, 2048, 1152)],
+    [(0, 768, 0), (768, 768, 128), (1536, 512, 320)],
 ]
-OUT_PIECES = [[768, 768, 512], [768, 640, 288, 224, 128]]
+OUT_PIECES = [[768, 768, 512], [960, 640, 320, 128]]
 
 
 def tile_picked_unmerge_relu_e_kernel(tc, xT, w1_words, w1_scales, res, offs, own, out):
@@ -42,13 +42,13 @@ def tile_picked_unmerge_relu_e_kernel(tc, xT, w1_words, w1_scales, res, offs, ow
         own_sb = keep.tile([P, U // 16], U16, name="own_sb")
         w_words = keep.tile([P, PASSES, 2 * N], U8, name="w_words", align_bytes=64)
         w_scales = keep.tile([P, PASSES, N], U8, name="w_scales", align_bytes=64)
-        nc.gpsimd.memset(w_scales[:].bitcast(I32), 0)
+        nc.vector.memset(w_scales[:].bitcast(I32), 0)
 
         x_rows = xT.rearrange("(z p u j) t -> z u p j t", z=PASSES, p=P, u=2, j=2)
         raw = {}
         for q in range(4):
             for (t0, width, vshare) in LOADS[q]:
-                raw[q, t0] = keep.tile([P, 2, width], F32, name="raw_%d_%d" % (q, t0), tag="raw_%d_%d" % (q, t0))
+                raw[q, t0] = keep.tile([P, 2, width], F32, name="raw_%d_%d" % (q, t0))
                 nc.sync.dma_start(raw[q, t0][:], x_rows[q // 2, q % 2][:, :, t0 : t0 + width])
                 if q == 0:
                     nc.sync.dma_start(offs_sb[:], offs)
@@ -59,8 +59,12 @@ def tile_picked_unmerge_relu_e_kernel(tc, xT, w1_words, w1_scales, res, offs, ow
             )
         nc.sync.dma_start(w_words[:].bitcast(I32), w1_words.rearrange("z p c -> p z c").bitcast(I32))
         nc.sync.dma_start(own_sb[:], own)
+        res_sb = []
+        for b in range(BLOCKS):
+            res_sb.append(keep.tile([P, U], F32, name="res_%d" % b))
+            nc.sync.dma_start(res_sb[b][:], res[b * P : (b + 1) * P, :])
 
-        pairs = [keep.tile([P, 2 * T], BF16, name="pairs_%d" % q, tag="pairs_%d" % q) for q in range(4)]
+        pairs = [keep.tile([P, 2 * T], BF16, name="pairs_%d" % q) for q in range(4)]
         picked = [keep.tile([P, 4 * S], BF16, name="picked_%d" % z) for z in range(PASSES)]
         woven = [keep.tile([P, 4 * S], BF16, name="woven_%d" % z, align_bytes=64) for z in range(PASSES)]
         codes = [keep.tile([P, S], U32, name="codes_%d" % z, align_bytes=64) for z in range(PASSES)]
@@ -133,10 +137,6 @@ def tile_picked_unmerge_relu_e_kernel(tc, xT, w1_words, w1_scales, res, offs, ow
             else:
                 weave(1, e0, SMALL)
                 weave(1, e0 + SMALL, SMALL)
-        res_sb = []
-        for b, tag in enumerate(["raw_3_%d" % LOADS[3][-1][0], "pairs_3"]):
-            res_sb.append(keep.tile([P, U], F32, name="res_%d" % b, tag=tag))
-            nc.sync.dma_start(res_sb[b][:], res[b * P : (b + 1) * P, :])
         for e0 in range(0, S - PIECE, PIECE):
             quantize(1, e0, PIECE)
         quantize(1, S - PIECE, SMALL)
@@ -144,7 +144,7 @@ def tile_picked_unmerge_relu_e_kernel(tc, xT, w1_words, w1_scales, res, offs, ow
         for g in range(8):
             multiply(g, 0, g * SMALL, SMALL, 1)
         for g in range(8):
-            if g == 7:
+            if g in (4, 5, 7):
                 nc.vector.tensor_scalar_max(y[0][:, g * SMALL : (g + 1) * SMALL], banks[g][:, :SMALL], 0.0)
             else:
                 nc.scalar.activation(y[0][:, g * SMALL : (g + 1) * SMALL], banks[g][:, :SMALL], ACT.Relu)

@@ -24,10 +24,10 @@ HALF = 512
 SMALL = 128
 
 LOADS = [
-    [(0, 2048, 1280)],
-    [(0, 1024, 0), (1024, 1024, 640)],
-    [(0, 2048, 1152)],
-    [(0, 768, 0), (768, 768, 128), (1536, 512, 320)],
+    [],
+    [(0, 1408, 1088), (1408, 640, 400)],
+    [(0, 2048, 1184)],
+    [(0, 768, 0), (768, 768, 192), (1536, 512, 288)],
 ]
 OUT_PIECES = [[768, 768, 512], [960, 640, 320, 128]]
 
@@ -46,12 +46,16 @@ def tile_picked_unmerge_relu_e_kernel(tc, xT, w1_words, w1_scales, res, offs, ow
 
         x_rows = xT.rearrange("(z p u j) t -> z u p j t", z=PASSES, p=P, u=2, j=2)
         raw = {}
-        for q in range(4):
+        planes = []
+        for j in range(2):
+            planes.append(keep.tile([P, T], F32, name="plane_%d" % j))
+            nc.sync.dma_start(planes[j][:], x_rows[0, 0][:, j, :])
+            if j == 0:
+                nc.sync.dma_start(offs_sb[:], offs)
+        for q in range(1, 4):
             for (t0, width, vshare) in LOADS[q]:
                 raw[q, t0] = keep.tile([P, 2, width], F32, name="raw_%d_%d" % (q, t0))
                 nc.sync.dma_start(raw[q, t0][:], x_rows[q // 2, q % 2][:, :, t0 : t0 + width])
-                if q == 0:
-                    nc.sync.dma_start(offs_sb[:], offs)
         for quad in range(4):
             nc.sync.dma_start(
                 w_scales[32 * quad : 32 * quad + 4, :, :].bitcast(I32),
@@ -64,7 +68,7 @@ def tile_picked_unmerge_relu_e_kernel(tc, xT, w1_words, w1_scales, res, offs, ow
             res_sb.append(keep.tile([P, U], F32, name="res_%d" % b))
             nc.sync.dma_start(res_sb[b][:], res[b * P : (b + 1) * P, :])
 
-        pairs = [keep.tile([P, 2 * T], BF16, name="pairs_%d" % q) for q in range(4)]
+        pairs = [None] + [keep.tile([P, 2 * T], BF16, name="pairs_%d" % q) for q in range(1, 4)]
         picked = [keep.tile([P, 4 * S], BF16, name="picked_%d" % z) for z in range(PASSES)]
         woven = [keep.tile([P, 4 * S], BF16, name="woven_%d" % z, align_bytes=64) for z in range(PASSES)]
         codes = [keep.tile([P, S], U32, name="codes_%d" % z, align_bytes=64) for z in range(PASSES)]
@@ -117,8 +121,19 @@ def tile_picked_unmerge_relu_e_kernel(tc, xT, w1_words, w1_scales, res, offs, ow
             dst, src = weave_views(z, e0, n, U32)
             nc.scalar.copy(dst, src)
 
-        cast(0)
-        gather(0, 0, S)
+        picked_planes = [keep.tile([P, 2, PIECE], F32, name="picked_planes_%d" % i) for i in range(S // PIECE)]
+        for j in range(2):
+            for i in range(S // PIECE):
+                e0 = i * PIECE
+                nc.vector.tensor_copy(
+                    picked_planes[i][:, j, :], planes[j][:].indirect(offs_sb[:, e0 // 16 : (e0 + PIECE) // 16])
+                )
+                if j == 1:
+                    nc.scalar.activation(
+                        picked[0][:, 2 * e0 : 2 * (e0 + PIECE)].rearrange("p (e j) -> p e j", j=2),
+                        picked_planes[i][:].rearrange("p j e -> p e j"),
+                        ACT.Copy,
+                    )
         cast(1)
         for e0 in range(0, S, PIECE):
             gather(1, e0, PIECE)
@@ -144,7 +159,7 @@ def tile_picked_unmerge_relu_e_kernel(tc, xT, w1_words, w1_scales, res, offs, ow
         for g in range(8):
             multiply(g, 0, g * SMALL, SMALL, 1)
         for g in range(8):
-            if g in (4, 5, 7):
+            if g in (4, 5, 6):
                 nc.vector.tensor_scalar_max(y[0][:, g * SMALL : (g + 1) * SMALL], banks[g][:, :SMALL], 0.0)
             else:
                 nc.scalar.activation(y[0][:, g * SMALL : (g + 1) * SMALL], banks[g][:, :SMALL], ACT.Relu)

@@ -24,12 +24,13 @@ HALF = 512
 SMALL = 128
 
 LOADS = [
-    [],
-    [(0, 1408, 1088), (1408, 640, 400)],
-    [(0, 2048, 1184)],
-    [(0, 768, 0), (768, 768, 192), (1536, 512, 288)],
+    [(0, 1152, 768), (1152, 896, 576)],
+    [(0, 768, 448), (768, 768, 528), (1536, 512, 320)],
+    [(0, 2048, 1200)],
+    [(0, 384, 0), (384, 896, 0), (1280, 768, 768)],
 ]
-OUT_PIECES = [[768, 768, 512], [960, 640, 320, 128]]
+SPARE = 128
+OUT_PIECES = [[1024, 1024], [1024, 576, 320, 128]]
 
 
 def tile_picked_unmerge_relu_e_kernel(tc, xT, w1_words, w1_scales, res, offs, own, out):
@@ -46,16 +47,14 @@ def tile_picked_unmerge_relu_e_kernel(tc, xT, w1_words, w1_scales, res, offs, ow
 
         x_rows = xT.rearrange("(z p u j) t -> z u p j t", z=PASSES, p=P, u=2, j=2)
         raw = {}
-        planes = []
-        for j in range(2):
-            planes.append(keep.tile([P, T], F32, name="plane_%d" % j))
-            nc.sync.dma_start(planes[j][:], x_rows[0, 0][:, j, :])
-            if j == 0:
-                nc.sync.dma_start(offs_sb[:], offs)
-        for q in range(1, 4):
+        for q in range(4):
+            raw[q] = keep.tile([P, 2 * T], F32, name="raw_%d" % q)
+            run = x_rows[q // 2, q % 2].rearrange("p j t -> p (j t)")
             for (t0, width, vshare) in LOADS[q]:
-                raw[q, t0] = keep.tile([P, 2, width], F32, name="raw_%d_%d" % (q, t0))
-                nc.sync.dma_start(raw[q, t0][:], x_rows[q // 2, q % 2][:, :, t0 : t0 + width])
+                first = T + t0 if t0 else 0
+                nc.sync.dma_start(raw[q][:, first : T + t0 + width], run[:, first : T + t0 + width])
+            if q == 0:
+                nc.sync.dma_start(offs_sb[:], offs)
         for quad in range(4):
             nc.sync.dma_start(
                 w_scales[32 * quad : 32 * quad + 4, :, :].bitcast(I32),
@@ -68,7 +67,7 @@ def tile_picked_unmerge_relu_e_kernel(tc, xT, w1_words, w1_scales, res, offs, ow
             res_sb.append(keep.tile([P, U], F32, name="res_%d" % b))
             nc.sync.dma_start(res_sb[b][:], res[b * P : (b + 1) * P, :])
 
-        pairs = [None] + [keep.tile([P, 2 * T], BF16, name="pairs_%d" % q) for q in range(1, 4)]
+        pairs = [keep.tile([P, 2 * T], BF16, name="pairs_%d" % q) for q in range(4)]
         picked = [keep.tile([P, 4 * S], BF16, name="picked_%d" % z) for z in range(PASSES)]
         woven = [keep.tile([P, 4 * S], BF16, name="woven_%d" % z, align_bytes=64) for z in range(PASSES)]
         codes = [keep.tile([P, S], U32, name="codes_%d" % z, align_bytes=64) for z in range(PASSES)]
@@ -76,7 +75,7 @@ def tile_picked_unmerge_relu_e_kernel(tc, xT, w1_words, w1_scales, res, offs, ow
 
         def cast(q):
             for (t0, width, on_vector) in LOADS[q]:
-                src = raw[q, t0][:].rearrange("p j t -> p t j")
+                src = raw[q][:].rearrange("p (j t) -> p t j", j=2)[:, t0 : t0 + width, :]
                 dst = pairs[q][:, 2 * t0 : 2 * (t0 + width)].rearrange("p (t j) -> p t j", j=2)
                 on_scalar = width - on_vector
                 if on_vector:
@@ -104,7 +103,9 @@ def tile_picked_unmerge_relu_e_kernel(tc, xT, w1_words, w1_scales, res, offs, ow
             )
 
         banks = [psum.tile([P, HALF], F32, name="bank_%d" % g) for g in range(8)]
-        y = [keep.tile([P, S], F32, name="y_%d" % b) for b in range(BLOCKS)]
+        y = [keep.tile([P, S + SPARE], F32, name="y_%d" % b) for b in range(BLOCKS)]
+        for b in range(BLOCKS):
+            nc.vector.memset(y[b][:, S:], 0.0)
 
         def multiply(bank, b, e0, n, z):
             nc.tensor.matmul_mx(
@@ -121,25 +122,15 @@ def tile_picked_unmerge_relu_e_kernel(tc, xT, w1_words, w1_scales, res, offs, ow
             dst, src = weave_views(z, e0, n, U32)
             nc.scalar.copy(dst, src)
 
-        picked_planes = [keep.tile([P, 2, PIECE], F32, name="picked_planes_%d" % i) for i in range(S // PIECE)]
-        for j in range(2):
-            for i in range(S // PIECE):
-                e0 = i * PIECE
-                nc.vector.tensor_copy(
-                    picked_planes[i][:, j, :], planes[j][:].indirect(offs_sb[:, e0 // 16 : (e0 + PIECE) // 16])
-                )
-                if j == 1:
-                    nc.scalar.activation(
-                        picked[0][:, 2 * e0 : 2 * (e0 + PIECE)].rearrange("p (e j) -> p e j", j=2),
-                        picked_planes[i][:].rearrange("p j e -> p e j"),
-                        ACT.Copy,
-                    )
+        cast(0)
+        gather(0, 0, S)
         cast(1)
         for e0 in range(0, S, PIECE):
             gather(1, e0, PIECE)
             weave(0, e0, PIECE)
-        for e0 in range(0, S, HALF):
-            quantize(0, e0, HALF)
+        quantize(0, 0, HALF)
+        for e0 in range(HALF, S, PIECE):
+            quantize(0, e0, PIECE)
         cast(2)
         gather(2, 0, S)
         for g in range(8):

@@ -24,10 +24,10 @@ HALF = 512
 SMALL = 128
 
 LOADS = [
-    [(0, 1152, 768), (1152, 896, 576)],
-    [(0, 768, 448), (768, 768, 528), (1536, 512, 320)],
-    [(0, 2048, 1200)],
-    [(0, 384, 0), (384, 896, 0), (1280, 768, 768)],
+    [(0, 1152, 768), (1152, 896, 544)],
+    [(0, 768, 448), (768, 768, 528), (1536, 512, 288)],
+    [(0, 2048, 1184)],
+    [(0, 832, 0), (832, 768, 360), (1600, 448, 256)],
 ]
 SPARE = 128
 OUT_PIECES = [[1024, 1024], [1024, 576, 320, 128]]
@@ -48,11 +48,18 @@ def tile_picked_unmerge_relu_e_kernel(tc, xT, w1_words, w1_scales, res, offs, ow
         x_rows = xT.rearrange("(z p u j) t -> z u p j t", z=PASSES, p=P, u=2, j=2)
         raw = {}
         for q in range(4):
-            raw[q] = keep.tile([P, 2 * T], F32, name="raw_%d" % q)
-            run = x_rows[q // 2, q % 2].rearrange("p j t -> p (j t)")
+            rows = x_rows[q // 2, q % 2]
+            if q < 3:
+                whole = keep.tile([P, 2 * T], F32, name="raw_%d" % q)
             for (t0, width, vshare) in LOADS[q]:
-                first = T + t0 if t0 else 0
-                nc.sync.dma_start(raw[q][:, first : T + t0 + width], run[:, first : T + t0 + width])
+                if q < 3:
+                    run = slice(T + t0 if t0 else 0, T + t0 + width)
+                    nc.sync.dma_start(whole[:, run], rows.rearrange("p j t -> p (j t)")[:, run])
+                    raw[q, t0] = whole[:].rearrange("p (j t) -> p j t", j=2)[:, :, t0 : t0 + width]
+                else:
+                    part = keep.tile([P, 2, width], F32, name="raw_%d_%d" % (q, t0))
+                    nc.sync.dma_start(part[:], rows[:, :, t0 : t0 + width])
+                    raw[q, t0] = part[:]
             if q == 0:
                 nc.sync.dma_start(offs_sb[:], offs)
         for quad in range(4):
@@ -62,9 +69,8 @@ def tile_picked_unmerge_relu_e_kernel(tc, xT, w1_words, w1_scales, res, offs, ow
             )
         nc.sync.dma_start(w_words[:].bitcast(I32), w1_words.rearrange("z p c -> p z c").bitcast(I32))
         nc.sync.dma_start(own_sb[:], own)
-        res_sb = []
+        res_sb = [keep.tile([P, U], F32, name="res_%d" % b) for b in range(BLOCKS)]
         for b in range(BLOCKS):
-            res_sb.append(keep.tile([P, U], F32, name="res_%d" % b))
             nc.sync.dma_start(res_sb[b][:], res[b * P : (b + 1) * P, :])
 
         pairs = [keep.tile([P, 2 * T], BF16, name="pairs_%d" % q) for q in range(4)]
@@ -73,9 +79,9 @@ def tile_picked_unmerge_relu_e_kernel(tc, xT, w1_words, w1_scales, res, offs, ow
         codes = [keep.tile([P, S], U32, name="codes_%d" % z, align_bytes=64) for z in range(PASSES)]
         scales = [keep.tile([P, S], U8, name="scales_%d" % z, align_bytes=64) for z in range(PASSES)]
 
-        def cast(q):
-            for (t0, width, on_vector) in LOADS[q]:
-                src = raw[q][:].rearrange("p (j t) -> p t j", j=2)[:, t0 : t0 + width, :]
+        def cast(q, loads):
+            for (t0, width, on_vector) in loads:
+                src = raw[q, t0].rearrange("p j t -> p t j")
                 dst = pairs[q][:, 2 * t0 : 2 * (t0 + width)].rearrange("p (t j) -> p t j", j=2)
                 on_scalar = width - on_vector
                 if on_vector:
@@ -122,20 +128,20 @@ def tile_picked_unmerge_relu_e_kernel(tc, xT, w1_words, w1_scales, res, offs, ow
             dst, src = weave_views(z, e0, n, U32)
             nc.scalar.copy(dst, src)
 
-        cast(0)
+        cast(0, LOADS[0])
         gather(0, 0, S)
-        cast(1)
+        cast(1, LOADS[1])
         for e0 in range(0, S, PIECE):
             gather(1, e0, PIECE)
             weave(0, e0, PIECE)
         quantize(0, 0, HALF)
         for e0 in range(HALF, S, PIECE):
             quantize(0, e0, PIECE)
-        cast(2)
+        cast(2, LOADS[2])
         gather(2, 0, S)
         for g in range(8):
             multiply(g, 0, g * SMALL, SMALL, 0)
-        cast(3)
+        cast(3, LOADS[3])
         for e0 in range(0, S, PIECE):
             gather(3, e0, PIECE)
             if e0 + PIECE < S:

@@ -30,7 +30,7 @@ LOADS = [
     [(0, 832, 0), (832, 768, 360), (1600, 448, 256)],
 ]
 SPARE = 128
-OUT_PIECES = [[1024, 1024], [1024, 576, 320, 128]]
+OUT_PIECES = [[1024, 1024], [768, 576, 448, 256]]
 
 
 def tile_picked_unmerge_relu_e_kernel(tc, xT, w1_words, w1_scales, res, offs, own, out):

@@ -15,6 +15,7 @@ FP8X4 = mybir.dt.float8_e4m3fn_x4
 FP4X4 = mybir.dt.float4_e2m1fn_x4
 ACT = mybir.ActivationFunctionType
 ADD = mybir.AluOpType.add
+MULT = mybir.AluOpType.mult
 
 P = 128
 PASSES = 2
@@ -23,14 +24,13 @@ PIECE = 256
 HALF = 512
 SMALL = 128
 
-LOADS = [
-    [(0, 1152, 768), (1152, 896, 544)],
-    [(0, 768, 448), (768, 768, 528), (1536, 512, 288)],
-    [(0, 2048, 1184)],
-    [(0, 832, 0), (832, 768, 360), (1600, 448, 256)],
-]
+PAIR_LOADS = [[[1152, 768], [896, 544]], [[768, 448], [768, 528], [512, 288]]]
+ROW3_LOADS = [[768, 768], [1280, 1152]]
+ROW2_LOADS = [[1024, 1024], [1024, 512]]
+SHARED_ON_VECTOR = 320
+VECTOR_BANKS = [4, 5, 6]
 SPARE = 128
-OUT_PIECES = [[1024, 1024], [768, 576, 448, 256]]
+OUT_PIECES = [[1024, 1024], [1088, 672, 288]]
 
 
 def tile_picked_unmerge_relu_e_kernel(tc, xT, w1_words, w1_scales, res, offs, own, out):
@@ -45,23 +45,29 @@ def tile_picked_unmerge_relu_e_kernel(tc, xT, w1_words, w1_scales, res, offs, ow
         w_scales = keep.tile([P, PASSES, N], U8, name="w_scales", align_bytes=64)
         nc.vector.memset(w_scales[:].bitcast(I32), 0)
 
-        x_rows = xT.rearrange("(z p u j) t -> z u p j t", z=PASSES, p=P, u=2, j=2)
-        raw = {}
-        for q in range(4):
-            rows = x_rows[q // 2, q % 2]
-            if q < 3:
-                whole = keep.tile([P, 2 * T], F32, name="raw_%d" % q)
-            for (t0, width, vshare) in LOADS[q]:
-                if q < 3:
-                    run = slice(T + t0 if t0 else 0, T + t0 + width)
-                    nc.sync.dma_start(whole[:, run], rows.rearrange("p j t -> p (j t)")[:, run])
-                    raw[q, t0] = whole[:].rearrange("p (j t) -> p j t", j=2)[:, :, t0 : t0 + width]
-                else:
-                    part = keep.tile([P, 2, width], F32, name="raw_%d_%d" % (q, t0))
-                    nc.sync.dma_start(part[:], rows[:, :, t0 : t0 + width])
-                    raw[q, t0] = part[:]
-            if q == 0:
+        x_rows = xT.rearrange("(z p j) t -> z p (j t)", z=PASSES, p=P, j=4)
+        raw = [keep.tile([P, 2 * T], F32, name="raw_%d" % u) for u in range(2)]
+        for u in range(2):
+            t0 = 0
+            for (width, on_vector) in PAIR_LOADS[u]:
+                run = slice(T + t0 if t0 else 0, T + t0 + width)
+                nc.sync.dma_start(raw[u][:, run], x_rows[0, :, 2 * T * u : 2 * T * (u + 1)][:, run])
+                t0 = t0 + width
+            if u == 0:
                 nc.sync.dma_start(offs_sb[:], offs)
+        row3 = keep.tile([P, T], F32, name="row3")
+        t0 = 0
+        for (width, on_gpsimd) in ROW3_LOADS:
+            nc.sync.dma_start(row3[:, t0 : t0 + width], x_rows[1, :, 3 * T + t0 : 3 * T + t0 + width])
+            t0 = t0 + width
+        rows12 = keep.tile([P, 2 * T], F32, name="rows12")
+        t0 = 0
+        for (width, on_gpsimd) in ROW2_LOADS:
+            run = slice(T + t0 if t0 else 0, T + t0 + width)
+            nc.sync.dma_start(rows12[:, run], x_rows[1, :, T : 3 * T][:, run])
+            t0 = t0 + width
+        row0 = keep.tile([P, T], F32, name="row0")
+        nc.sync.dma_start(row0[:], x_rows[1, :, :T])
         for quad in range(4):
             nc.sync.dma_start(
                 w_scales[32 * quad : 32 * quad + 4, :, :].bitcast(I32),
@@ -73,33 +79,47 @@ def tile_picked_unmerge_relu_e_kernel(tc, xT, w1_words, w1_scales, res, offs, ow
         for b in range(BLOCKS):
             nc.sync.dma_start(res_sb[b][:], res[b * P : (b + 1) * P, :])
 
-        pairs = [keep.tile([P, 2 * T], BF16, name="pairs_%d" % q) for q in range(4)]
+        pairs = [keep.tile([P, 2 * T], BF16, name="pairs_%d" % u) for u in range(2)]
+        row3_bf = keep.tile([P, T], BF16, name="row3_bf")
+        row2_bf = keep.tile([P, T], BF16, name="row2_bf")
         picked = [keep.tile([P, 4 * S], BF16, name="picked_%d" % z) for z in range(PASSES)]
         woven = [keep.tile([P, 4 * S], BF16, name="woven_%d" % z, align_bytes=64) for z in range(PASSES)]
         codes = [keep.tile([P, S], U32, name="codes_%d" % z, align_bytes=64) for z in range(PASSES)]
         scales = [keep.tile([P, S], U8, name="scales_%d" % z, align_bytes=64) for z in range(PASSES)]
 
-        def cast(q, loads):
-            for (t0, width, on_vector) in loads:
-                src = raw[q, t0].rearrange("p j t -> p t j")
-                dst = pairs[q][:, 2 * t0 : 2 * (t0 + width)].rearrange("p (t j) -> p t j", j=2)
+        def entries(e0, n):
+            return offs_sb[:, e0 // 16 : (e0 + n) // 16]
+
+        def round_pair(u):
+            t0 = 0
+            for (width, on_vector) in PAIR_LOADS[u]:
+                src = raw[u][:].rearrange("p (j t) -> p t j", j=2)[:, t0 : t0 + width, :]
+                dst = pairs[u][:, 2 * t0 : 2 * (t0 + width)].rearrange("p (t j) -> p t j", j=2)
                 on_scalar = width - on_vector
-                if on_vector:
-                    nc.vector.tensor_copy(
-                        dst[:, on_scalar:, :].rearrange("p (c i) j -> p c j i", i=4),
-                        src[:, on_scalar:, :].rearrange("p (c i) j -> p c j i", i=4),
-                    )
-                if on_scalar:
-                    nc.scalar.activation(dst[:, :on_scalar, :], src[:, :on_scalar, :], ACT.Copy)
+                nc.vector.tensor_copy(dst[:, on_scalar:, :], src[:, on_scalar:, :])
+                nc.scalar.activation(dst[:, :on_scalar, :], src[:, :on_scalar, :], ACT.Copy)
+                t0 = t0 + width
 
-        def gather(q, e0, n):
-            dst = picked[q // 2][:].bitcast(U32)[:, (q % 2) * S + e0 : (q % 2) * S + e0 + n]
-            nc.vector.tensor_copy(dst, pairs[q][:].bitcast(U32).indirect(offs_sb[:, e0 // 16 : (e0 + n) // 16]))
+        def round_row(dst, src, loads):
+            t0 = 0
+            for (width, on_gpsimd) in loads:
+                t1 = t0 + on_gpsimd
+                nc.gpsimd.tensor_scalar(dst[:, t0:t1], src[:, t0:t1], 1.0, 0.0, MULT, ADD)
+                if on_gpsimd < width:
+                    nc.scalar.activation(dst[:, t1 : t0 + width], src[:, t1 : t0 + width], ACT.Copy)
+                t0 = t0 + width
 
-        def weave_views(z, e0, n, dt):
-            src = picked[z][:].bitcast(dt).rearrange("p (u e) -> p e u", u=2)[:, e0 : e0 + n, :]
-            dst = woven[z][:].bitcast(dt)[:, 2 * e0 : 2 * (e0 + n)].rearrange("p (e u) -> p e u", u=2)
-            return dst, src
+        def gather_pair(u, e0, n):
+            dst = picked[0][:].bitcast(U32)[:, u * S + e0 : u * S + e0 + n]
+            nc.vector.tensor_copy(dst, pairs[u][:].bitcast(U32).indirect(entries(e0, n)))
+
+        def slot(j, e0, n):
+            return picked[1][:].rearrange("p (u e i) -> p u e i", u=2, i=2)[:, j // 2, e0 : e0 + n, j % 2]
+
+        def weave(z, e0, n):
+            src = picked[z][:].bitcast(U32).rearrange("p (u e) -> p e u", u=2)[:, e0 : e0 + n, :]
+            dst = woven[z][:].bitcast(U32)[:, 2 * e0 : 2 * (e0 + n)].rearrange("p (e u) -> p e u", u=2)
+            nc.scalar.copy(dst, src)
 
         def quantize(z, e0, n):
             nc.vector.quantize_mx(
@@ -124,26 +144,28 @@ def tile_picked_unmerge_relu_e_kernel(tc, xT, w1_words, w1_scales, res, offs, ow
                 stop=(z == PASSES - 1),
             )
 
-        def weave(z, e0, n):
-            dst, src = weave_views(z, e0, n, U32)
-            nc.scalar.copy(dst, src)
-
-        cast(0, LOADS[0])
-        gather(0, 0, S)
-        cast(1, LOADS[1])
+        round_pair(0)
+        gather_pair(0, 0, S)
+        round_pair(1)
         for e0 in range(0, S, PIECE):
-            gather(1, e0, PIECE)
+            gather_pair(1, e0, PIECE)
             weave(0, e0, PIECE)
         quantize(0, 0, HALF)
         for e0 in range(HALF, S, PIECE):
             quantize(0, e0, PIECE)
-        cast(2, LOADS[2])
-        gather(2, 0, S)
+
+        mine, rest = SHARED_ON_VECTOR, S - SHARED_ON_VECTOR
+        round_row(row3_bf, row3, ROW3_LOADS)
+        nc.vector.tensor_copy(slot(3, 0, mine), row3[:].indirect(entries(0, mine)))
+        nc.scalar.activation(slot(3, mine, rest), row3_bf[:].indirect(entries(mine, rest)), ACT.Copy)
+        nc.vector.tensor_copy(slot(1, 0, S), rows12[:, :T].indirect(entries(0, S)))
+        round_row(row2_bf, rows12[:, T:], ROW2_LOADS)
+        nc.vector.tensor_copy(slot(2, 0, mine), rows12[:, T:].indirect(entries(0, mine)))
+        nc.scalar.activation(slot(2, mine, rest), row2_bf[:].indirect(entries(mine, rest)), ACT.Copy)
         for g in range(8):
             multiply(g, 0, g * SMALL, SMALL, 0)
-        cast(3, LOADS[3])
         for e0 in range(0, S, PIECE):
-            gather(3, e0, PIECE)
+            nc.vector.tensor_copy(slot(0, e0, PIECE), row0[:].indirect(entries(e0, PIECE)))
             if e0 + PIECE < S:
                 weave(1, e0, PIECE)
             else:
@@ -156,7 +178,7 @@ def tile_picked_unmerge_relu_e_kernel(tc, xT, w1_words, w1_scales, res, offs, ow
         for g in range(8):
             multiply(g, 0, g * SMALL, SMALL, 1)
         for g in range(8):
-            if g in (4, 5, 6):
+            if g in VECTOR_BANKS:
                 nc.vector.tensor_scalar_max(y[0][:, g * SMALL : (g + 1) * SMALL], banks[g][:, :SMALL], 0.0)
             else:
                 nc.scalar.activation(y[0][:, g * SMALL : (g + 1) * SMALL], banks[g][:, :SMALL], ACT.Relu)

@@ -24,9 +24,9 @@ PIECE = 256
 HALF = 512
 SMALL = 128
 
-PAIR_LOADS = [[[1152, 768], [896, 544]], [[768, 448], [768, 528], [512, 288]]]
-ROW3_LOADS = [[768, 768], [1280, 1152]]
-ROW2_LOADS = [[1024, 1024], [1024, 512]]
+PAIR_LOADS = [[[1152, 704], [896, 544]], [[768, 384], [768, 480], [512, 296]]]
+ROW3_LOADS = [[896, 896], [1152, 1024]]
+ROW2_LOADS = [[768, 768], [1280, 576]]
 SHARED_ON_VECTOR = 320
 VECTOR_BANKS = [4, 5, 6]
 SPARE = 128
@@ -81,9 +81,8 @@ def tile_picked_unmerge_relu_e_kernel(tc, xT, w1_words, w1_scales, res, offs, ow
 
         pairs = [keep.tile([P, 2 * T], BF16, name="pairs_%d" % u) for u in range(2)]
         row3_bf = keep.tile([P, T], BF16, name="row3_bf")
-        row2_bf = keep.tile([P, T], BF16, name="row2_bf")
         picked = [keep.tile([P, 4 * S], BF16, name="picked_%d" % z) for z in range(PASSES)]
-        woven = [keep.tile([P, 4 * S], BF16, name="woven_%d" % z, align_bytes=64) for z in range(PASSES)]
+        woven = [keep.tile([P, 4 * S], BF16, name="woven_%d" % z, tag="woven_%d" % z, align_bytes=64) for z in range(PASSES)]
         codes = [keep.tile([P, S], U32, name="codes_%d" % z, align_bytes=64) for z in range(PASSES)]
         scales = [keep.tile([P, S], U8, name="scales_%d" % z, align_bytes=64) for z in range(PASSES)]
 
@@ -159,6 +158,7 @@ def tile_picked_unmerge_relu_e_kernel(tc, xT, w1_words, w1_scales, res, offs, ow
         nc.vector.tensor_copy(slot(3, 0, mine), row3[:].indirect(entries(0, mine)))
         nc.scalar.activation(slot(3, mine, rest), row3_bf[:].indirect(entries(mine, rest)), ACT.Copy)
         nc.vector.tensor_copy(slot(1, 0, S), rows12[:, :T].indirect(entries(0, S)))
+        row2_bf = keep.tile([P, T], BF16, name="row2_bf", tag="woven_0", align_bytes=64)
         round_row(row2_bf, rows12[:, T:], ROW2_LOADS)
         nc.vector.tensor_copy(slot(2, 0, mine), rows12[:, T:].indirect(entries(0, mine)))
         nc.scalar.activation(slot(2, mine, rest), row2_bf[:].indirect(entries(mine, rest)), ACT.Copy)

@@ -28,9 +28,10 @@ PAIR_LOADS = [[[1152, 704], [896, 544]], [[768, 384], [768, 480], [512, 296]]]
 ROW3_LOADS = [[896, 896], [1152, 1024]]
 ROW2_LOADS = [[768, 768], [1280, 576]]
 SHARED_ON_VECTOR = 320
-VECTOR_BANKS = [4, 5, 6]
+GROUPS = [256, 256, 256, 128, 128]
+VECTOR_GROUP = 2
 SPARE = 128
-OUT_PIECES = [[1024, 1024], [1088, 672, 288]]
+OUT_PIECES = [[1024, 1024], [832, 544, 352, 192, 128]]
 
 
 def tile_picked_unmerge_relu_e_kernel(tc, xT, w1_words, w1_scales, res, offs, own, out):
@@ -73,11 +74,16 @@ def tile_picked_unmerge_relu_e_kernel(tc, xT, w1_words, w1_scales, res, offs, ow
                 w_scales[32 * quad : 32 * quad + 4, :, :].bitcast(I32),
                 w1_scales[:, 4 * quad : 4 * quad + 4, :].rearrange("z r c -> r z c").bitcast(I32),
             )
-        nc.sync.dma_start(w_words[:].bitcast(I32), w1_words.rearrange("z p c -> p z c").bitcast(I32))
+        for z in range(PASSES):
+            nc.sync.dma_start(w_words[:, z, :].bitcast(I32), w1_words[z].bitcast(I32))
         nc.sync.dma_start(own_sb[:], own)
-        res_sb = [keep.tile([P, U], F32, name="res_%d" % b) for b in range(BLOCKS)]
+        res_sb = {}
         for b in range(BLOCKS):
-            nc.sync.dma_start(res_sb[b][:], res[b * P : (b + 1) * P, :])
+            r0 = 0
+            for n in OUT_PIECES[b]:
+                res_sb[b, r0] = keep.tile([P, n], F32, name="res_%d_%d" % (b, r0))
+                nc.sync.dma_start(res_sb[b, r0][:], res[b * P : (b + 1) * P, r0 : r0 + n])
+                r0 = r0 + n
 
         pairs = [keep.tile([P, 2 * T], BF16, name="pairs_%d" % u) for u in range(2)]
         row3_bf = keep.tile([P, T], BF16, name="row3_bf")
@@ -127,20 +133,21 @@ def tile_picked_unmerge_relu_e_kernel(tc, xT, w1_words, w1_scales, res, offs, ow
                 in_=woven[z][:, 4 * e0 : 4 * (e0 + n)],
             )
 
-        banks = [psum.tile([P, HALF], F32, name="bank_%d" % g) for g in range(8)]
+        banks = [psum.tile([P, HALF], F32, name="bank_%d" % g) for g in range(5)]
         y = [keep.tile([P, S + SPARE], F32, name="y_%d" % b) for b in range(BLOCKS)]
         for b in range(BLOCKS):
             nc.vector.memset(y[b][:, S:], 0.0)
 
-        def multiply(bank, b, e0, n, z):
+        def multiply(sums, b, e0, z, start, stop):
+            n = sums.shape[1]
             nc.tensor.matmul_mx(
-                out=banks[bank][:, :n],
+                out=sums,
                 lhsT=w_words[:, z, 2 * P * b : 2 * P * (b + 1)].bitcast(FP4X4),
                 lhsT_scale=w_scales[:, z, P * b : P * (b + 1)],
                 rhs=codes[z][:, e0 : e0 + n].bitcast(FP8X4),
                 rhs_scale=scales[z][:, e0 : e0 + n],
-                start=(z == 0),
-                stop=(z == PASSES - 1),
+                start=start,
+                stop=stop,
             )
 
         round_pair(0)
@@ -162,8 +169,10 @@ def tile_picked_unmerge_relu_e_kernel(tc, xT, w1_words, w1_scales, res, offs, ow
         round_row(row2_bf, rows12[:, T:], ROW2_LOADS)
         nc.vector.tensor_copy(slot(2, 0, mine), rows12[:, T:].indirect(entries(0, mine)))
         nc.scalar.activation(slot(2, mine, rest), row2_bf[:].indirect(entries(mine, rest)), ACT.Copy)
-        for g in range(8):
-            multiply(g, 0, g * SMALL, SMALL, 0)
+        firsts = [sum(GROUPS[:g]) for g in range(len(GROUPS))]
+        for g, n in enumerate(GROUPS):
+            for c0 in range(0, n, SMALL):
+                multiply(banks[g][:, c0 : c0 + SMALL], 0, firsts[g] + c0, 0, c0 == 0, False)
         for e0 in range(0, S, PIECE):
             nc.vector.tensor_copy(slot(0, e0, PIECE), row0[:].indirect(entries(e0, PIECE)))
             if e0 + PIECE < S:
@@ -175,24 +184,25 @@ def tile_picked_unmerge_relu_e_kernel(tc, xT, w1_words, w1_scales, res, offs, ow
             quantize(1, e0, PIECE)
         quantize(1, S - PIECE, SMALL)
         quantize(1, S - SMALL, SMALL)
-        for g in range(8):
-            multiply(g, 0, g * SMALL, SMALL, 1)
-        for g in range(8):
-            if g in VECTOR_BANKS:
-                nc.vector.tensor_scalar_max(y[0][:, g * SMALL : (g + 1) * SMALL], banks[g][:, :SMALL], 0.0)
+        for g, n in enumerate(GROUPS):
+            for c0 in range(0, n, SMALL):
+                multiply(banks[g][:, c0 : c0 + SMALL], 0, firsts[g] + c0, 1, False, c0 + SMALL == n)
+        for g, n in enumerate(GROUPS):
+            if g == VECTOR_GROUP:
+                nc.vector.tensor_scalar_max(y[0][:, firsts[g] : firsts[g] + n], banks[g][:, :n], 0.0)
             else:
-                nc.scalar.activation(y[0][:, g * SMALL : (g + 1) * SMALL], banks[g][:, :SMALL], ACT.Relu)
+                nc.scalar.activation(y[0][:, firsts[g] : firsts[g] + n], banks[g][:, :n], ACT.Relu)
         for h in range(2):
             for z in range(PASSES):
-                multiply(6 + h, 1, h * HALF, HALF, z)
-            nc.scalar.activation(y[1][:, h * HALF : (h + 1) * HALF], banks[6 + h][:], ACT.Relu)
+                multiply(banks[3 + h][:], 1, h * HALF, z, z == 0, z == PASSES - 1)
+            nc.scalar.activation(y[1][:, h * HALF : (h + 1) * HALF], banks[3 + h][:], ACT.Relu)
 
         for b in range(BLOCKS):
             r0 = 0
             for n in OUT_PIECES[b]:
                 summed = keep.tile([P, n], F32, name="summed_%d_%d" % (b, r0))
                 nc.vector.tensor_tensor(
-                    summed[:], y[b][:].indirect(own_sb[:, r0 // 16 : (r0 + n) // 16]), res_sb[b][:, r0 : r0 + n], ADD
+                    summed[:], y[b][:].indirect(own_sb[:, r0 // 16 : (r0 + n) // 16]), res_sb[b, r0][:], ADD
                 )
                 nc.sync.dma_start(out[b * P : (b + 1) * P, r0 : r0 + n], summed[:])
                 r0 = r0 + n

@@ -31,6 +31,7 @@ SHARED_ON_VECTOR = 320
 GROUPS = [256, 256, 256, 128, 128]
 VECTOR_GROUP = 2
 SPARE = 128
+RES_LOADS = [[1024, 1024], [832, 544, 352, 320]]
 OUT_PIECES = [[1024, 1024], [832, 544, 352, 192, 128]]
 
 
@@ -74,16 +75,17 @@ def tile_picked_unmerge_relu_e_kernel(tc, xT, w1_words, w1_scales, res, offs, ow
                 w_scales[32 * quad : 32 * quad + 4, :, :].bitcast(I32),
                 w1_scales[:, 4 * quad : 4 * quad + 4, :].rearrange("z r c -> r z c").bitcast(I32),
             )
-        for z in range(PASSES):
-            nc.sync.dma_start(w_words[:, z, :].bitcast(I32), w1_words[z].bitcast(I32))
+        nc.sync.dma_start(w_words[:, 0, :].bitcast(I32), w1_words[0].bitcast(I32))
+        nc.sync.dma_start(w_words[:, 1, : 2 * P].bitcast(I32), w1_words[1, :, : 2 * P].bitcast(I32))
         nc.sync.dma_start(own_sb[:], own)
-        res_sb = {}
+        res_sb = [keep.tile([P, U], F32, name="res_%d" % b) for b in range(BLOCKS)]
         for b in range(BLOCKS):
             r0 = 0
-            for n in OUT_PIECES[b]:
-                res_sb[b, r0] = keep.tile([P, n], F32, name="res_%d_%d" % (b, r0))
-                nc.sync.dma_start(res_sb[b, r0][:], res[b * P : (b + 1) * P, r0 : r0 + n])
+            for n in RES_LOADS[b]:
+                nc.sync.dma_start(res_sb[b][:, r0 : r0 + n], res[b * P : (b + 1) * P, r0 : r0 + n])
                 r0 = r0 + n
+                if b == 1 and r0 == sum(RES_LOADS[1][:2]):
+                    nc.sync.dma_start(w_words[:, 1, 2 * P :].bitcast(I32), w1_words[1, :, 2 * P :].bitcast(I32))
 
         pairs = [keep.tile([P, 2 * T], BF16, name="pairs_%d" % u) for u in range(2)]
         row3_bf = keep.tile([P, T], BF16, name="row3_bf")
@@ -133,7 +135,7 @@ def tile_picked_unmerge_relu_e_kernel(tc, xT, w1_words, w1_scales, res, offs, ow
                 in_=woven[z][:, 4 * e0 : 4 * (e0 + n)],
             )
 
-        banks = [psum.tile([P, HALF], F32, name="bank_%d" % g) for g in range(5)]
+        banks = [psum.tile([P, HALF], F32, name="bank_%d" % g) for g in range(7)]
         y = [keep.tile([P, S + SPARE], F32, name="y_%d" % b) for b in range(BLOCKS)]
         for b in range(BLOCKS):
             nc.vector.memset(y[b][:, S:], 0.0)
@@ -173,6 +175,8 @@ def tile_picked_unmerge_relu_e_kernel(tc, xT, w1_words, w1_scales, res, offs, ow
         for g, n in enumerate(GROUPS):
             for c0 in range(0, n, SMALL):
                 multiply(banks[g][:, c0 : c0 + SMALL], 0, firsts[g] + c0, 0, c0 == 0, False)
+        for h in range(2):
+            multiply(banks[5 + h][:], 1, h * HALF, 0, True, False)
         for e0 in range(0, S, PIECE):
             nc.vector.tensor_copy(slot(0, e0, PIECE), row0[:].indirect(entries(e0, PIECE)))
             if e0 + PIECE < S:
@@ -193,16 +197,15 @@ def tile_picked_unmerge_relu_e_kernel(tc, xT, w1_words, w1_scales, res, offs, ow
             else:
                 nc.scalar.activation(y[0][:, firsts[g] : firsts[g] + n], banks[g][:, :n], ACT.Relu)
         for h in range(2):
-            for z in range(PASSES):
-                multiply(banks[3 + h][:], 1, h * HALF, z, z == 0, z == PASSES - 1)
-            nc.scalar.activation(y[1][:, h * HALF : (h + 1) * HALF], banks[3 + h][:], ACT.Relu)
+            multiply(banks[5 + h][:], 1, h * HALF, 1, False, True)
+            nc.scalar.activation(y[1][:, h * HALF : (h + 1) * HALF], banks[5 + h][:], ACT.Relu)
 
         for b in range(BLOCKS):
             r0 = 0
             for n in OUT_PIECES[b]:
                 summed = keep.tile([P, n], F32, name="summed_%d_%d" % (b, r0))
                 nc.vector.tensor_tensor(
-                    summed[:], y[b][:].indirect(own_sb[:, r0 // 16 : (r0 + n) // 16]), res_sb[b, r0][:], ADD
+                    summed[:], y[b][:].indirect(own_sb[:, r0 // 16 : (r0 + n) // 16]), res_sb[b][:, r0 : r0 + n], ADD
                 )
                 nc.sync.dma_start(out[b * P : (b + 1) * P, r0 : r0 + n], summed[:])
                 r0 = r0 + n

@@ -27,7 +27,7 @@ SMALL = 128
 PAIR_LOADS = [[[1152, 704], [896, 544]], [[768, 384], [768, 480], [512, 296]]]
 ROW3_LOADS = [[896, 896], [1152, 1024]]
 ROW2_LOADS = [[768, 768], [1280, 576]]
-SHARED_ON_VECTOR = 320
+SHARED_ON_VECTOR = 256
 GROUPS = [256, 256, 256, 128, 128]
 VECTOR_GROUP = 2
 SPARE = 128

@@ -24,14 +24,11 @@ PIECE = 256
 HALF = 512
 SMALL = 128
 
-PAIR_LOADS = [[[1152, 704], [896, 544]], [[768, 384], [768, 480], [512, 296]]]
-ROW3_LOADS = [[896, 896], [1152, 1024]]
-ROW2_LOADS = [[768, 768], [1280, 576]]
-SHARED_ON_VECTOR = 256
+SHARED_ON_VECTOR = [448, 256]
+ROUNDED = {(0, 0): [(T, 960)], (0, 1): [(T, 1408)], (1, 3): [[896, 896], [1152, 1088]], (1, 2): [[768, 768], [1280, 576]]}
 GROUPS = [256, 256, 256, 128, 128]
 VECTOR_GROUP = 2
 SPARE = 128
-RES_LOADS = [[1024, 1024], [832, 544, 352, 320]]
 OUT_PIECES = [[1024, 1024], [832, 544, 352, 192, 128]]
 
 
@@ -48,47 +45,44 @@ def tile_picked_unmerge_relu_e_kernel(tc, xT, w1_words, w1_scales, res, offs, ow
         nc.vector.memset(w_scales[:].bitcast(I32), 0)
 
         x_rows = xT.rearrange("(z p j) t -> z p (j t)", z=PASSES, p=P, j=4)
-        raw = [keep.tile([P, 2 * T], F32, name="raw_%d" % u) for u in range(2)]
-        for u in range(2):
-            t0 = 0
-            for (width, on_vector) in PAIR_LOADS[u]:
-                run = slice(T + t0 if t0 else 0, T + t0 + width)
-                nc.sync.dma_start(raw[u][:, run], x_rows[0, :, 2 * T * u : 2 * T * (u + 1)][:, run])
-                t0 = t0 + width
-            if u == 0:
-                nc.sync.dma_start(offs_sb[:], offs)
-        row3 = keep.tile([P, T], F32, name="row3")
-        t0 = 0
-        for (width, on_gpsimd) in ROW3_LOADS:
-            nc.sync.dma_start(row3[:, t0 : t0 + width], x_rows[1, :, 3 * T + t0 : 3 * T + t0 + width])
-            t0 = t0 + width
-        rows12 = keep.tile([P, 2 * T], F32, name="rows12")
-        t0 = 0
-        for (width, on_gpsimd) in ROW2_LOADS:
-            run = slice(T + t0 if t0 else 0, T + t0 + width)
-            nc.sync.dma_start(rows12[:, run], x_rows[1, :, T : 3 * T][:, run])
-            t0 = t0 + width
-        row0 = keep.tile([P, T], F32, name="row0")
-        nc.sync.dma_start(row0[:], x_rows[1, :, :T])
+        raw = [keep.tile([P, 4 * T], F32, name="raw_%d" % z) for z in range(PASSES)]
+
+        def load_x(z, c0, c1):
+            nc.sync.dma_start(raw[z][:, c0:c1], x_rows[z, :, c0:c1])
+
+        def load_words(z, b):
+            cols = slice(2 * P * b, 2 * P * (b + 1))
+            nc.sync.dma_start(w_words[:, z, cols].bitcast(I32), w1_words[z, :, cols].bitcast(I32))
+
+        load_x(0, 0, 2 * T)
+        nc.sync.dma_start(offs_sb[:], offs)
+        load_x(0, 2 * T, 3 * T)
+        load_x(0, 3 * T, 4 * T)
+        cut3 = 3 * T + ROUNDED[1, 3][0][0]
+        cut2 = 2 * T + ROUNDED[1, 2][0][0]
+        load_x(1, 3 * T, cut3)
+        load_x(1, cut3, 4 * T)
+        load_x(1, T, cut2)
+        load_x(1, cut2, 3 * T)
+        load_x(1, 0, T)
         for quad in range(4):
             nc.sync.dma_start(
                 w_scales[32 * quad : 32 * quad + 4, :, :].bitcast(I32),
                 w1_scales[:, 4 * quad : 4 * quad + 4, :].rearrange("z r c -> r z c").bitcast(I32),
             )
-        nc.sync.dma_start(w_words[:, 0, :].bitcast(I32), w1_words[0].bitcast(I32))
-        nc.sync.dma_start(w_words[:, 1, : 2 * P].bitcast(I32), w1_words[1, :, : 2 * P].bitcast(I32))
+        load_words(0, 0)
+        load_words(0, 1)
+        load_words(1, 0)
         nc.sync.dma_start(own_sb[:], own)
         res_sb = [keep.tile([P, U], F32, name="res_%d" % b) for b in range(BLOCKS)]
         for b in range(BLOCKS):
             r0 = 0
-            for n in RES_LOADS[b]:
+            for n in OUT_PIECES[b]:
                 nc.sync.dma_start(res_sb[b][:, r0 : r0 + n], res[b * P : (b + 1) * P, r0 : r0 + n])
                 r0 = r0 + n
-                if b == 1 and r0 == sum(RES_LOADS[1][:2]):
-                    nc.sync.dma_start(w_words[:, 1, 2 * P :].bitcast(I32), w1_words[1, :, 2 * P :].bitcast(I32))
+                if b == 1 and r0 == sum(OUT_PIECES[1][:2]):
+                    load_words(1, 1)
 
-        pairs = [keep.tile([P, 2 * T], BF16, name="pairs_%d" % u) for u in range(2)]
-        row3_bf = keep.tile([P, T], BF16, name="row3_bf")
         picked = [keep.tile([P, 4 * S], BF16, name="picked_%d" % z) for z in range(PASSES)]
         woven = [keep.tile([P, 4 * S], BF16, name="woven_%d" % z, tag="woven_%d" % z, align_bytes=64) for z in range(PASSES)]
         codes = [keep.tile([P, S], U32, name="codes_%d" % z, align_bytes=64) for z in range(PASSES)]
@@ -97,31 +91,24 @@ def tile_picked_unmerge_relu_e_kernel(tc, xT, w1_words, w1_scales, res, offs, ow
         def entries(e0, n):
             return offs_sb[:, e0 // 16 : (e0 + n) // 16]
 
-        def round_pair(u):
-            t0 = 0
-            for (width, on_vector) in PAIR_LOADS[u]:
-                src = raw[u][:].rearrange("p (j t) -> p t j", j=2)[:, t0 : t0 + width, :]
-                dst = pairs[u][:, 2 * t0 : 2 * (t0 + width)].rearrange("p (t j) -> p t j", j=2)
-                on_scalar = width - on_vector
-                nc.vector.tensor_copy(dst[:, on_scalar:, :], src[:, on_scalar:, :])
-                nc.scalar.activation(dst[:, :on_scalar, :], src[:, :on_scalar, :], ACT.Copy)
-                t0 = t0 + width
+        def halves(z, j, e0, n):
+            return picked[z][:].rearrange("p (u e i) -> p u e i", u=2, i=2)[:, j // 2, e0 : e0 + n, j % 2]
 
-        def round_row(dst, src, loads):
+        def gather_on_vector(z, j, e0, n):
+            nc.vector.tensor_copy(halves(z, j, e0, n), raw[z][:, j * T : (j + 1) * T].indirect(entries(e0, n)))
+
+        def gather_shared(z, j, rounded):
+            row = raw[z][:, j * T : (j + 1) * T]
             t0 = 0
-            for (width, on_gpsimd) in loads:
+            for (width, on_gpsimd) in ROUNDED[z, j]:
                 t1 = t0 + on_gpsimd
-                nc.gpsimd.tensor_scalar(dst[:, t0:t1], src[:, t0:t1], 1.0, 0.0, MULT, ADD)
+                nc.gpsimd.tensor_scalar(rounded[:, t0:t1], row[:, t0:t1], 1.0, 0.0, MULT, ADD)
                 if on_gpsimd < width:
-                    nc.scalar.activation(dst[:, t1 : t0 + width], src[:, t1 : t0 + width], ACT.Copy)
+                    nc.scalar.activation(rounded[:, t1 : t0 + width], row[:, t1 : t0 + width], ACT.Copy)
                 t0 = t0 + width
-
-        def gather_pair(u, e0, n):
-            dst = picked[0][:].bitcast(U32)[:, u * S + e0 : u * S + e0 + n]
-            nc.vector.tensor_copy(dst, pairs[u][:].bitcast(U32).indirect(entries(e0, n)))
-
-        def slot(j, e0, n):
-            return picked[1][:].rearrange("p (u e i) -> p u e i", u=2, i=2)[:, j // 2, e0 : e0 + n, j % 2]
+            mine = SHARED_ON_VECTOR[z]
+            gather_on_vector(z, j, 0, mine)
+            nc.scalar.activation(halves(z, j, mine, S - mine), rounded[:].indirect(entries(mine, S - mine)), ACT.Copy)
 
         def weave(z, e0, n):
             src = picked[z][:].bitcast(U32).rearrange("p (u e) -> p e u", u=2)[:, e0 : e0 + n, :]
@@ -135,7 +122,7 @@ def tile_picked_unmerge_relu_e_kernel(tc, xT, w1_words, w1_scales, res, offs, ow
                 in_=woven[z][:, 4 * e0 : 4 * (e0 + n)],
             )
 
-        banks = [psum.tile([P, HALF], F32, name="bank_%d" % g) for g in range(7)]
+        banks = [psum.tile([P, HALF], F32, name="bank_%d" % g) for g in range(len(GROUPS) + 2)]
         y = [keep.tile([P, S + SPARE], F32, name="y_%d" % b) for b in range(BLOCKS)]
         for b in range(BLOCKS):
             nc.vector.memset(y[b][:, S:], 0.0)
@@ -152,42 +139,34 @@ def tile_picked_unmerge_relu_e_kernel(tc, xT, w1_words, w1_scales, res, offs, ow
                 stop=stop,
             )
 
-        round_pair(0)
-        gather_pair(0, 0, S)
-        round_pair(1)
+        for j in (0, 1):
+            gather_shared(0, j, keep.tile([P, T], BF16, name="rounded_0_%d" % j))
+        gather_on_vector(0, 2, 0, S)
         for e0 in range(0, S, PIECE):
-            gather_pair(1, e0, PIECE)
+            gather_on_vector(0, 3, e0, PIECE)
             weave(0, e0, PIECE)
         quantize(0, 0, HALF)
         for e0 in range(HALF, S, PIECE):
             quantize(0, e0, PIECE)
 
-        mine, rest = SHARED_ON_VECTOR, S - SHARED_ON_VECTOR
-        round_row(row3_bf, row3, ROW3_LOADS)
-        nc.vector.tensor_copy(slot(3, 0, mine), row3[:].indirect(entries(0, mine)))
-        nc.scalar.activation(slot(3, mine, rest), row3_bf[:].indirect(entries(mine, rest)), ACT.Copy)
-        nc.vector.tensor_copy(slot(1, 0, S), rows12[:, :T].indirect(entries(0, S)))
-        row2_bf = keep.tile([P, T], BF16, name="row2_bf", tag="woven_0", align_bytes=64)
-        round_row(row2_bf, rows12[:, T:], ROW2_LOADS)
-        nc.vector.tensor_copy(slot(2, 0, mine), rows12[:, T:].indirect(entries(0, mine)))
-        nc.scalar.activation(slot(2, mine, rest), row2_bf[:].indirect(entries(mine, rest)), ACT.Copy)
+        gather_shared(1, 3, keep.tile([P, T], BF16, name="rounded_1_3"))
+        gather_on_vector(1, 1, 0, S)
+        gather_shared(1, 2, keep.tile([P, T], BF16, name="rounded_1_2", tag="woven_0", align_bytes=64))
         firsts = [sum(GROUPS[:g]) for g in range(len(GROUPS))]
         for g, n in enumerate(GROUPS):
             for c0 in range(0, n, SMALL):
                 multiply(banks[g][:, c0 : c0 + SMALL], 0, firsts[g] + c0, 0, c0 == 0, False)
         for h in range(2):
-            multiply(banks[5 + h][:], 1, h * HALF, 0, True, False)
+            multiply(banks[len(GROUPS) + h][:], 1, h * HALF, 0, True, False)
         for e0 in range(0, S, PIECE):
-            nc.vector.tensor_copy(slot(0, e0, PIECE), row0[:].indirect(entries(e0, PIECE)))
+            gather_on_vector(1, 0, e0, PIECE)
             if e0 + PIECE < S:
                 weave(1, e0, PIECE)
             else:
                 weave(1, e0, SMALL)
                 weave(1, e0 + SMALL, SMALL)
-        for e0 in range(0, S - PIECE, PIECE):
-            quantize(1, e0, PIECE)
-        quantize(1, S - PIECE, SMALL)
-        quantize(1, S - SMALL, SMALL)
+        for g, n in enumerate(GROUPS):
+            quantize(1, firsts[g], n)
         for g, n in enumerate(GROUPS):
             for c0 in range(0, n, SMALL):
                 multiply(banks[g][:, c0 : c0 + SMALL], 0, firsts[g] + c0, 1, False, c0 + SMALL == n)
@@ -197,8 +176,8 @@ def tile_picked_unmerge_relu_e_kernel(tc, xT, w1_words, w1_scales, res, offs, ow
             else:
                 nc.scalar.activation(y[0][:, firsts[g] : firsts[g] + n], banks[g][:, :n], ACT.Relu)
         for h in range(2):
-            multiply(banks[5 + h][:], 1, h * HALF, 1, False, True)
-            nc.scalar.activation(y[1][:, h * HALF : (h + 1) * HALF], banks[5 + h][:], ACT.Relu)
+            multiply(banks[len(GROUPS) + h][:], 1, h * HALF, 1, False, True)
+            nc.scalar.activation(y[1][:, h * HALF : (h + 1) * HALF], banks[len(GROUPS) + h][:], ACT.Relu)
 
         for b in range(BLOCKS):
             r0 = 0

@@ -15,21 +15,18 @@ FP8X4 = mybir.dt.float8_e4m3fn_x4
 FP4X4 = mybir.dt.float4_e2m1fn_x4
 ACT = mybir.ActivationFunctionType
 ADD = mybir.AluOpType.add
-MULT = mybir.AluOpType.mult
 
 P = 128
 PASSES = 2
 BLOCKS = 2
-PIECE = 256
 HALF = 512
-SMALL = 128
-
-SHARED_ON_VECTOR = [448, 256]
-ROUNDED = {(0, 0): [(T, 960)], (0, 1): [(T, 1408)], (1, 3): [[896, 896], [1152, 1088]], (1, 2): [[768, 768], [1280, 576]]}
+GAP = 16
+DIRECT = 256
+ROW5_ON_VECTOR = 256
 GROUPS = [256, 256, 256, 128, 128]
-VECTOR_GROUP = 2
-SPARE = 128
-OUT_PIECES = [[1024, 1024], [832, 544, 352, 192, 128]]
+FUSED = [(0, 0, 512), (0, 512, 512), (0, 1024, 256), (1, 0, 256), (1, 256, 128), (1, 384, 128)]
+FETCHED = [(0, 1280, 768), (1, 512, 512), (1, 1024, 512), (1, 1536, 320), (1, 1856, 192)]
+VECTOR_GROUPS = (2, 4)
 
 
 def tile_picked_unmerge_relu_e_kernel(tc, xT, w1_words, w1_scales, res, offs, own, out):
@@ -45,87 +42,39 @@ def tile_picked_unmerge_relu_e_kernel(tc, xT, w1_words, w1_scales, res, offs, ow
         nc.vector.memset(w_scales[:].bitcast(I32), 0)
 
         x_rows = xT.rearrange("(z p j) t -> z p (j t)", z=PASSES, p=P, j=4)
-        raw = [keep.tile([P, 4 * T], F32, name="raw_%d" % z) for z in range(PASSES)]
-
-        def load_x(z, c0, c1):
-            nc.sync.dma_start(raw[z][:, c0:c1], x_rows[z, :, c0:c1])
-
-        def load_words(z, b):
-            cols = slice(2 * P * b, 2 * P * (b + 1))
-            nc.sync.dma_start(w_words[:, z, cols].bitcast(I32), w1_words[z, :, cols].bitcast(I32))
-
-        load_x(0, 0, 2 * T)
+        two_rows = [keep.tile([P, 2 * T], F32, name="two_rows_%d" % u) for u in range(2)]
+        one_row = [keep.tile([P, T], F32, name="one_row_%d" % j) for j in range(4)]
+        nc.sync.dma_start(two_rows[0][:], x_rows[0, :, 0 : 2 * T])
         nc.sync.dma_start(offs_sb[:], offs)
-        load_x(0, 2 * T, 3 * T)
-        load_x(0, 3 * T, 4 * T)
-        cut3 = 3 * T + ROUNDED[1, 3][0][0]
-        cut2 = 2 * T + ROUNDED[1, 2][0][0]
-        load_x(1, 3 * T, cut3)
-        load_x(1, cut3, 4 * T)
-        load_x(1, T, cut2)
-        load_x(1, cut2, 3 * T)
-        load_x(1, 0, T)
+        nc.sync.dma_start(two_rows[1][:], x_rows[0, :, 2 * T : 4 * T])
+        for j in range(4):
+            nc.sync.dma_start(one_row[j][:], x_rows[1, :, j * T : (j + 1) * T])
         for quad in range(4):
             nc.sync.dma_start(
                 w_scales[32 * quad : 32 * quad + 4, :, :].bitcast(I32),
                 w1_scales[:, 4 * quad : 4 * quad + 4, :].rearrange("z r c -> r z c").bitcast(I32),
             )
-        load_words(0, 0)
-        load_words(0, 1)
-        load_words(1, 0)
+        nc.sync.dma_start(w_words[:].bitcast(I32), w1_words.rearrange("z p c -> p z c").bitcast(I32))
         nc.sync.dma_start(own_sb[:], own)
         res_sb = [keep.tile([P, U], F32, name="res_%d" % b) for b in range(BLOCKS)]
         for b in range(BLOCKS):
-            r0 = 0
-            for n in OUT_PIECES[b]:
-                nc.sync.dma_start(res_sb[b][:, r0 : r0 + n], res[b * P : (b + 1) * P, r0 : r0 + n])
-                r0 = r0 + n
-                if b == 1 and r0 == sum(OUT_PIECES[1][:2]):
-                    load_words(1, 1)
+            nc.sync.dma_start(res_sb[b][:], res[b * P : (b + 1) * P, :])
 
-        picked = [keep.tile([P, 4 * S], BF16, name="picked_%d" % z) for z in range(PASSES)]
-        woven = [keep.tile([P, 4 * S], BF16, name="woven_%d" % z, tag="woven_%d" % z, align_bytes=64) for z in range(PASSES)]
+        gapped = [keep.tile([P, 2, 2, HALF + GAP], BF16, name="gapped_%d" % u) for u in range(2)]
+        planes = [keep.tile([P, 2, S], BF16, name="planes_%d" % u) for u in range(2)]
+        woven = [keep.tile([P, S, 4], BF16, name="woven_%d" % z, align_bytes=64) for z in range(PASSES)]
         codes = [keep.tile([P, S], U32, name="codes_%d" % z, align_bytes=64) for z in range(PASSES)]
         scales = [keep.tile([P, S], U8, name="scales_%d" % z, align_bytes=64) for z in range(PASSES)]
 
         def entries(e0, n):
             return offs_sb[:, e0 // 16 : (e0 + n) // 16]
 
-        def halves(z, j, e0, n):
-            return picked[z][:].rearrange("p (u e i) -> p u e i", u=2, i=2)[:, j // 2, e0 : e0 + n, j % 2]
-
-        def gather_on_vector(z, j, e0, n):
-            nc.vector.tensor_copy(halves(z, j, e0, n), raw[z][:, j * T : (j + 1) * T].indirect(entries(e0, n)))
-
-        def gather_shared(z, j, rounded):
-            row = raw[z][:, j * T : (j + 1) * T]
-            t0 = 0
-            for (width, on_gpsimd) in ROUNDED[z, j]:
-                t1 = t0 + on_gpsimd
-                nc.gpsimd.tensor_scalar(rounded[:, t0:t1], row[:, t0:t1], 1.0, 0.0, MULT, ADD)
-                if on_gpsimd < width:
-                    nc.scalar.activation(rounded[:, t1 : t0 + width], row[:, t1 : t0 + width], ACT.Copy)
-                t0 = t0 + width
-            mine = SHARED_ON_VECTOR[z]
-            gather_on_vector(z, j, 0, mine)
-            nc.scalar.activation(halves(z, j, mine, S - mine), rounded[:].indirect(entries(mine, S - mine)), ACT.Copy)
-
-        def weave(z, e0, n):
-            src = picked[z][:].bitcast(U32).rearrange("p (u e) -> p e u", u=2)[:, e0 : e0 + n, :]
-            dst = woven[z][:].bitcast(U32)[:, 2 * e0 : 2 * (e0 + n)].rearrange("p (e u) -> p e u", u=2)
-            nc.scalar.copy(dst, src)
-
         def quantize(z, e0, n):
             nc.vector.quantize_mx(
                 out=codes[z][:, e0 : e0 + n].bitcast(FP8X4),
                 scales=scales[z][:, e0 : e0 + n],
-                in_=woven[z][:, 4 * e0 : 4 * (e0 + n)],
+                in_=woven[z][:, e0 : e0 + n, :].rearrange("p e j -> p (e j)"),
             )
-
-        banks = [psum.tile([P, HALF], F32, name="bank_%d" % g) for g in range(len(GROUPS) + 2)]
-        y = [keep.tile([P, S + SPARE], F32, name="y_%d" % b) for b in range(BLOCKS)]
-        for b in range(BLOCKS):
-            nc.vector.memset(y[b][:, S:], 0.0)
 
         def multiply(sums, b, e0, z, start, stop):
             n = sums.shape[1]
@@ -139,52 +88,99 @@ def tile_picked_unmerge_relu_e_kernel(tc, xT, w1_words, w1_scales, res, offs, ow
                 stop=stop,
             )
 
-        for j in (0, 1):
-            gather_shared(0, j, keep.tile([P, T], BF16, name="rounded_0_%d" % j))
-        gather_on_vector(0, 2, 0, S)
-        for e0 in range(0, S, PIECE):
-            gather_on_vector(0, 3, e0, PIECE)
-            weave(0, e0, PIECE)
-        quantize(0, 0, HALF)
-        for e0 in range(HALF, S, PIECE):
-            quantize(0, e0, PIECE)
+        for u in range(2):
+            for h in range(2):
+                nc.scalar.activation(gapped[u][:, 0, h, :HALF], two_rows[u][:].indirect(entries(h * HALF, HALF)), ACT.Copy)
+            nc.vector.tensor_copy(gapped[u][:, 1, :, :HALF], two_rows[u][:, T:].indirect(offs_sb[:]))
+            for h in range(2):
+                nc.vector.tensor_copy(
+                    woven[0][:, h * HALF : (h + 1) * HALF, 2 * u : 2 * u + 2],
+                    gapped[u][:, :, h, :HALF].rearrange("p j e -> p e j"),
+                )
+        for h in range(2):
+            quantize(0, h * HALF, HALF)
 
-        gather_shared(1, 3, keep.tile([P, T], BF16, name="rounded_1_3"))
-        gather_on_vector(1, 1, 0, S)
-        gather_shared(1, 2, keep.tile([P, T], BF16, name="rounded_1_2", tag="woven_0", align_bytes=64))
+        def on_scalar(j, e0, n):
+            nc.scalar.activation(planes[j // 2][:, j % 2, e0 : e0 + n], one_row[j][:].indirect(entries(e0, n)), ACT.Copy)
+
+        def place(u, e0, n):
+            nc.vector.tensor_copy(
+                woven[1][:, e0 : e0 + n, 2 * u : 2 * u + 2], planes[u][:, :, e0 : e0 + n].rearrange("p j e -> p e j")
+            )
+
+        def direct(j, e0, n):
+            nc.vector.tensor_copy(woven[1][:, e0 : e0 + n, j], one_row[j][:].indirect(entries(e0, n)))
+
+        on_scalar(0, 0, S)
+        on_scalar(1, 0, HALF)
+        on_scalar(1, HALF, S - HALF - ROW5_ON_VECTOR)
+        nc.vector.tensor_copy(
+            planes[0][:, 1, S - ROW5_ON_VECTOR :], one_row[1][:].indirect(entries(S - ROW5_ON_VECTOR, ROW5_ON_VECTOR))
+        )
+        place(0, 0, HALF)
+        place(0, HALF, HALF)
+        on_scalar(2, DIRECT, S - DIRECT)
+        direct(2, 0, DIRECT)
+
+        banks = [psum.tile([P, HALF], F32, name="bank_%d" % g) for g in range(len(GROUPS) + 2)]
+        y = [keep.tile([P, S], F32, name="y_%d" % b) for b in range(BLOCKS)]
         firsts = [sum(GROUPS[:g]) for g in range(len(GROUPS))]
         for g, n in enumerate(GROUPS):
-            for c0 in range(0, n, SMALL):
-                multiply(banks[g][:, c0 : c0 + SMALL], 0, firsts[g] + c0, 0, c0 == 0, False)
+            multiply(banks[g][:, :n], 0, firsts[g], 0, True, False)
+        wide = banks[len(GROUPS) :]
+
+        def finish(g):
+            e0, n = firsts[g], GROUPS[g]
+            quantize(1, e0, n)
+            multiply(banks[g][:, :n], 0, e0, 1, False, True)
+
+        direct(3, 0, DIRECT)
+        for e0 in range(DIRECT, S, 256):
+            on_scalar(3, e0, 256)
+        place(1, 256, 256)
+        finish(0)
+        place(1, 512, 256)
+        finish(1)
+        nc.scalar.copy(woven[1][:, 768:, 2:4], planes[1][:, :, 768:].rearrange("p j e -> p e j"))
+        finish(2)
+        finish(3)
+        finish(4)
         for h in range(2):
-            multiply(banks[len(GROUPS) + h][:], 1, h * HALF, 0, True, False)
-        for e0 in range(0, S, PIECE):
-            gather_on_vector(1, 0, e0, PIECE)
-            if e0 + PIECE < S:
-                weave(1, e0, PIECE)
-            else:
-                weave(1, e0, SMALL)
-                weave(1, e0 + SMALL, SMALL)
+            for z in range(PASSES):
+                multiply(wide[h][:], 1, h * HALF, z, z == 0, z == 1)
         for g, n in enumerate(GROUPS):
-            quantize(1, firsts[g], n)
-        for g, n in enumerate(GROUPS):
-            for c0 in range(0, n, SMALL):
-                multiply(banks[g][:, c0 : c0 + SMALL], 0, firsts[g] + c0, 1, False, c0 + SMALL == n)
-        for g, n in enumerate(GROUPS):
-            if g == VECTOR_GROUP:
+            if g in VECTOR_GROUPS:
                 nc.vector.tensor_scalar_max(y[0][:, firsts[g] : firsts[g] + n], banks[g][:, :n], 0.0)
             else:
                 nc.scalar.activation(y[0][:, firsts[g] : firsts[g] + n], banks[g][:, :n], ACT.Relu)
-        for h in range(2):
-            multiply(banks[len(GROUPS) + h][:], 1, h * HALF, 1, False, True)
-            nc.scalar.activation(y[1][:, h * HALF : (h + 1) * HALF], banks[len(GROUPS) + h][:], ACT.Relu)
 
-        for b in range(BLOCKS):
-            r0 = 0
-            for n in OUT_PIECES[b]:
-                summed = keep.tile([P, n], F32, name="summed_%d_%d" % (b, r0))
-                nc.vector.tensor_tensor(
-                    summed[:], y[b][:].indirect(own_sb[:, r0 // 16 : (r0 + n) // 16]), res_sb[b][:, r0 : r0 + n], ADD
-                )
-                nc.sync.dma_start(out[b * P : (b + 1) * P, r0 : r0 + n], summed[:])
-                r0 = r0 + n
+        def owners(r0, n):
+            return own_sb[:, r0 // 16 : (r0 + n) // 16]
+
+        def fused(i):
+            b, r0, n = FUSED[i]
+            summed = keep.tile([P, n], F32, name="summed_0_%d" % i)
+            nc.vector.tensor_tensor(summed[:], y[b][:].indirect(owners(r0, n)), res_sb[b][:, r0 : r0 + n], ADD)
+            nc.sync.dma_start(out[b * P : (b + 1) * P, r0 : r0 + n], summed[:])
+
+        def added(i):
+            b, r0, n = FETCHED[i]
+            fetched = keep.tile([P, n], F32, name="fetched_%d" % i)
+            nc.scalar.activation(fetched[:], y[b][:].indirect(owners(r0, n)), ACT.Copy)
+            summed = keep.tile([P, n], F32, name="summed_1_%d" % i)
+            nc.vector.tensor_tensor(summed[:], fetched[:], res_sb[b][:, r0 : r0 + n], ADD)
+            nc.sync.dma_start(out[b * P : (b + 1) * P, r0 : r0 + n], summed[:])
+
+        fused(0)
+        fused(1)
+        added(0)
+        for h in range(2):
+            nc.scalar.activation(y[1][:, h * HALF : (h + 1) * HALF], wide[h][:], ACT.Relu)
+        fused(2)
+        fused(3)
+        added(1)
+        fused(4)
+        added(2)
+        fused(5)
+        added(3)
+        added(4)

@@ -20,13 +20,11 @@ P = 128
 PASSES = 2
 BLOCKS = 2
 HALF = 512
-GAP = 16
 DIRECT = 256
-ROW5_ON_VECTOR = 256
+ON_VECTOR = [[512, 640, 256, 576], [0, 448, 128]]
 GROUPS = [256, 256, 256, 128, 128]
-FUSED = [(0, 0, 512), (0, 512, 512), (0, 1024, 256), (1, 0, 256), (1, 256, 128), (1, 384, 128)]
-FETCHED = [(0, 1280, 768), (1, 512, 512), (1, 1024, 512), (1, 1536, 320), (1, 1856, 192)]
 VECTOR_GROUPS = (2, 4)
+STORES = [(0, 512, 320), (0, 448, 384), (0, 384, 0), (1, 256, 384), (1, 128, 384), (1, 128, 256), (1, 192, 0), (1, 0, 192), (1, 128, 0)]
 
 
 def tile_picked_unmerge_relu_e_kernel(tc, xT, w1_words, w1_scales, res, offs, own, out):
@@ -41,14 +39,13 @@ def tile_picked_unmerge_relu_e_kernel(tc, xT, w1_words, w1_scales, res, offs, ow
         w_scales = keep.tile([P, PASSES, N], U8, name="w_scales", align_bytes=64)
         nc.vector.memset(w_scales[:].bitcast(I32), 0)
 
-        x_rows = xT.rearrange("(z p j) t -> z p (j t)", z=PASSES, p=P, j=4)
-        two_rows = [keep.tile([P, 2 * T], F32, name="two_rows_%d" % u) for u in range(2)]
-        one_row = [keep.tile([P, T], F32, name="one_row_%d" % j) for j in range(4)]
-        nc.sync.dma_start(two_rows[0][:], x_rows[0, :, 0 : 2 * T])
-        nc.sync.dma_start(offs_sb[:], offs)
-        nc.sync.dma_start(two_rows[1][:], x_rows[0, :, 2 * T : 4 * T])
-        for j in range(4):
-            nc.sync.dma_start(one_row[j][:], x_rows[1, :, j * T : (j + 1) * T])
+        x_rows = xT.rearrange("(z p j) t -> z j p t", z=PASSES, p=P, j=4)
+        rows = [[keep.tile([P, T], F32, name="row_%d_%d" % (z, j)) for j in range(4)] for z in range(PASSES)]
+        for z in range(PASSES):
+            for j in range(4):
+                nc.sync.dma_start(rows[z][j][:], x_rows[z, j])
+                if z == 0 and j == 0:
+                    nc.sync.dma_start(offs_sb[:], offs)
         for quad in range(4):
             nc.sync.dma_start(
                 w_scales[32 * quad : 32 * quad + 4, :, :].bitcast(I32),
@@ -60,14 +57,35 @@ def tile_picked_unmerge_relu_e_kernel(tc, xT, w1_words, w1_scales, res, offs, ow
         for b in range(BLOCKS):
             nc.sync.dma_start(res_sb[b][:], res[b * P : (b + 1) * P, :])
 
-        gapped = [keep.tile([P, 2, 2, HALF + GAP], BF16, name="gapped_%d" % u) for u in range(2)]
-        planes = [keep.tile([P, 2, S], BF16, name="planes_%d" % u) for u in range(2)]
+        planes = [[keep.tile([P, 2, S], BF16, name="planes_%d_%d" % (z, u)) for u in range(2)] for z in range(PASSES)]
         woven = [keep.tile([P, S, 4], BF16, name="woven_%d" % z, align_bytes=64) for z in range(PASSES)]
         codes = [keep.tile([P, S], U32, name="codes_%d" % z, align_bytes=64) for z in range(PASSES)]
         scales = [keep.tile([P, S], U8, name="scales_%d" % z, align_bytes=64) for z in range(PASSES)]
 
-        def entries(e0, n):
-            return offs_sb[:, e0 // 16 : (e0 + n) // 16]
+        def picked(z, j, e0, e1):
+            return rows[z][j][:].indirect(offs_sb[:, e0 // 16 : e1 // 16])
+
+        def on_scalar(z, j, e0, e1):
+            nc.scalar.activation(planes[z][j // 2][:, j % 2, e0:e1], picked(z, j, e0, e1), ACT.Copy)
+
+        def on_vector(z, j, e0, e1):
+            nc.vector.tensor_copy(planes[z][j // 2][:, j % 2, e0:e1], picked(z, j, e0, e1))
+
+        def shared(z, j, e0):
+            cut = S - ON_VECTOR[z][j]
+            on_scalar(z, j, e0, cut)
+            if cut < S:
+                on_vector(z, j, cut, S)
+            return cut
+
+        def pair(z, u, e0, e1):
+            return woven[z][:, e0:e1, 2 * u : 2 * u + 2], planes[z][u][:, :, e0:e1].rearrange("p j e -> p e j")
+
+        def place(z, u, e0, e1):
+            nc.vector.tensor_copy(*pair(z, u, e0, e1))
+
+        def direct(j):
+            nc.vector.tensor_copy(woven[1][:, :DIRECT, j], picked(1, j, 0, DIRECT))
 
         def quantize(z, e0, n):
             nc.vector.quantize_mx(
@@ -89,98 +107,66 @@ def tile_picked_unmerge_relu_e_kernel(tc, xT, w1_words, w1_scales, res, offs, ow
             )
 
         for u in range(2):
+            shared(0, 2 * u, 0)
+            shared(0, 2 * u + 1, 0)
             for h in range(2):
-                nc.scalar.activation(gapped[u][:, 0, h, :HALF], two_rows[u][:].indirect(entries(h * HALF, HALF)), ACT.Copy)
-            nc.vector.tensor_copy(gapped[u][:, 1, :, :HALF], two_rows[u][:, T:].indirect(offs_sb[:]))
-            for h in range(2):
-                nc.vector.tensor_copy(
-                    woven[0][:, h * HALF : (h + 1) * HALF, 2 * u : 2 * u + 2],
-                    gapped[u][:, :, h, :HALF].rearrange("p j e -> p e j"),
-                )
+                place(0, u, h * HALF, (h + 1) * HALF)
         for h in range(2):
             quantize(0, h * HALF, HALF)
 
-        def on_scalar(j, e0, n):
-            nc.scalar.activation(planes[j // 2][:, j % 2, e0 : e0 + n], one_row[j][:].indirect(entries(e0, n)), ACT.Copy)
+        shared(1, 0, 0)
+        cut = shared(1, 1, 0)
+        place(1, 0, cut, S)
+        place(1, 0, 0, cut)
+        shared(1, 2, DIRECT)
+        direct(2)
 
-        def place(u, e0, n):
-            nc.vector.tensor_copy(
-                woven[1][:, e0 : e0 + n, 2 * u : 2 * u + 2], planes[u][:, :, e0 : e0 + n].rearrange("p j e -> p e j")
-            )
-
-        def direct(j, e0, n):
-            nc.vector.tensor_copy(woven[1][:, e0 : e0 + n, j], one_row[j][:].indirect(entries(e0, n)))
-
-        on_scalar(0, 0, S)
-        on_scalar(1, 0, HALF)
-        on_scalar(1, HALF, S - HALF - ROW5_ON_VECTOR)
-        nc.vector.tensor_copy(
-            planes[0][:, 1, S - ROW5_ON_VECTOR :], one_row[1][:].indirect(entries(S - ROW5_ON_VECTOR, ROW5_ON_VECTOR))
-        )
-        place(0, 0, HALF)
-        place(0, HALF, HALF)
-        on_scalar(2, DIRECT, S - DIRECT)
-        direct(2, 0, DIRECT)
-
-        banks = [psum.tile([P, HALF], F32, name="bank_%d" % g) for g in range(len(GROUPS) + 2)]
+        banks = [psum.tile([P, HALF], F32, name="bank_%d" % g, tag="bank_%d" % g) for g in range(len(GROUPS))]
         y = [keep.tile([P, S], F32, name="y_%d" % b) for b in range(BLOCKS)]
         firsts = [sum(GROUPS[:g]) for g in range(len(GROUPS))]
         for g, n in enumerate(GROUPS):
             multiply(banks[g][:, :n], 0, firsts[g], 0, True, False)
-        wide = banks[len(GROUPS) :]
 
         def finish(g):
-            e0, n = firsts[g], GROUPS[g]
-            quantize(1, e0, n)
-            multiply(banks[g][:, :n], 0, e0, 1, False, True)
+            quantize(1, firsts[g], GROUPS[g])
+            multiply(banks[g][:, : GROUPS[g]], 0, firsts[g], 1, False, True)
 
-        direct(3, 0, DIRECT)
-        for e0 in range(DIRECT, S, 256):
-            on_scalar(3, e0, 256)
-        place(1, 256, 256)
-        finish(0)
-        place(1, 512, 256)
-        finish(1)
-        nc.scalar.copy(woven[1][:, 768:, 2:4], planes[1][:, :, 768:].rearrange("p j e -> p e j"))
-        finish(2)
-        finish(3)
-        finish(4)
-        for h in range(2):
-            for z in range(PASSES):
-                multiply(wide[h][:], 1, h * HALF, z, z == 0, z == 1)
+        direct(3)
+        for g in range(1, len(GROUPS)):
+            on_scalar(1, 3, firsts[g], firsts[g] + GROUPS[g])
+        nc.scalar.copy(*pair(1, 1, firsts[-1], S))
+        for g in range(1, len(GROUPS) - 1):
+            place(1, 1, firsts[g], firsts[g + 1])
+            finish(g - 1)
+        finish(len(GROUPS) - 2)
+        finish(len(GROUPS) - 1)
         for g, n in enumerate(GROUPS):
             if g in VECTOR_GROUPS:
                 nc.vector.tensor_scalar_max(y[0][:, firsts[g] : firsts[g] + n], banks[g][:, :n], 0.0)
             else:
                 nc.scalar.activation(y[0][:, firsts[g] : firsts[g] + n], banks[g][:, :n], ACT.Relu)
-
-        def owners(r0, n):
-            return own_sb[:, r0 // 16 : (r0 + n) // 16]
-
-        def fused(i):
-            b, r0, n = FUSED[i]
-            summed = keep.tile([P, n], F32, name="summed_0_%d" % i)
-            nc.vector.tensor_tensor(summed[:], y[b][:].indirect(owners(r0, n)), res_sb[b][:, r0 : r0 + n], ADD)
-            nc.sync.dma_start(out[b * P : (b + 1) * P, r0 : r0 + n], summed[:])
-
-        def added(i):
-            b, r0, n = FETCHED[i]
-            fetched = keep.tile([P, n], F32, name="fetched_%d" % i)
-            nc.scalar.activation(fetched[:], y[b][:].indirect(owners(r0, n)), ACT.Copy)
-            summed = keep.tile([P, n], F32, name="summed_1_%d" % i)
-            nc.vector.tensor_tensor(summed[:], fetched[:], res_sb[b][:, r0 : r0 + n], ADD)
-            nc.sync.dma_start(out[b * P : (b + 1) * P, r0 : r0 + n], summed[:])
-
-        fused(0)
-        fused(1)
-        added(0)
+        wide = [psum.tile([P, HALF], F32, name="wide_%d" % h, tag="bank_%d" % (2 + h)) for h in range(2)]
         for h in range(2):
-            nc.scalar.activation(y[1][:, h * HALF : (h + 1) * HALF], wide[h][:], ACT.Relu)
-        fused(2)
-        fused(3)
-        added(1)
-        fused(4)
-        added(2)
-        fused(5)
-        added(3)
-        added(4)
+            for z in range(PASSES):
+                multiply(wide[h][:], 1, h * HALF, z, z == 0, z == 1)
+
+        def owners(r0, r1):
+            return own_sb[:, r0 // 16 : r1 // 16]
+
+        done = [0] * BLOCKS
+        for i, (b, fused, apart) in enumerate(STORES):
+            if b == 1 and done[1] == 0:
+                for h in range(2):
+                    nc.scalar.activation(y[1][:, h * HALF : (h + 1) * HALF], wide[h][:], ACT.Relu)
+            r0 = done[b]
+            r1 = r0 + fused
+            r2 = r1 + apart
+            summed = keep.tile([P, r2 - r0], F32, name="summed_%d" % i)
+            if fused:
+                nc.vector.tensor_tensor(summed[:, :fused], y[b][:].indirect(owners(r0, r1)), res_sb[b][:, r0:r1], ADD)
+            if apart:
+                fetched = keep.tile([P, apart], F32, name="fetched_%d" % i)
+                nc.scalar.activation(fetched[:], y[b][:].indirect(owners(r1, r2)), ACT.Copy)
+                nc.vector.tensor_tensor(summed[:, fused:], fetched[:], res_sb[b][:, r1:r2], ADD)
+            nc.sync.dma_start(out[b * P : (b + 1) * P, r0:r2], summed[:])
+            done[b] = r2

@@ -24,7 +24,10 @@ DIRECT = 256
 ON_VECTOR = [[512, 640, 256, 576], [0, 448, 128]]
 GROUPS = [256, 256, 256, 128, 128]
 VECTOR_GROUPS = (2, 4)
-STORES = [(0, 512, 320), (0, 448, 384), (0, 384, 0), (1, 256, 384), (1, 128, 384), (1, 128, 256), (1, 192, 0), (1, 0, 192), (1, 128, 0)]
+STORES = [
+    (0, 576, 0), (0, 0, 384), (0, 640, 0), (0, 0, 448),
+    (1, 416, 0), (1, 0, 384), (1, 224, 0), (1, 0, 416), (1, 0, 224), (1, 128, 0), (1, 0, 128), (1, 128, 0),
+]
 
 
 def tile_picked_unmerge_relu_e_kernel(tc, xT, w1_words, w1_scales, res, offs, own, out):

@@ -22,11 +22,11 @@ BLOCKS = 2
 HALF = 512
 DIRECT = 256
 ON_VECTOR = [[512, 640, 256, 576], [0, 448, 128]]
-GROUPS = [256, 256, 256, 128, 128]
+GROUPS = [256, 256, 128, 128, 128, 128]
 VECTOR_GROUPS = (2, 4)
 STORES = [
     (0, 576, 0), (0, 0, 384), (0, 640, 0), (0, 0, 448),
-    (1, 416, 0), (1, 0, 384), (1, 224, 0), (1, 0, 416), (1, 0, 224), (1, 128, 0), (1, 0, 128), (1, 128, 0),
+    (1, 448, 0), (1, 0, 416), (1, 256, 0), (1, 0, 384), (1, 192, 0), (1, 0, 224), (1, 0, 128),
 ]
 
 
@@ -135,20 +135,21 @@ def tile_picked_unmerge_relu_e_kernel(tc, xT, w1_words, w1_scales, res, offs, ow
             multiply(banks[g][:, : GROUPS[g]], 0, firsts[g], 1, False, True)
 
         direct(3)
-        for g in range(1, len(GROUPS)):
-            on_scalar(1, 3, firsts[g], firsts[g] + GROUPS[g])
-        nc.scalar.copy(*pair(1, 1, firsts[-1], S))
-        for g in range(1, len(GROUPS) - 1):
-            place(1, 1, firsts[g], firsts[g + 1])
-            finish(g - 1)
-        finish(len(GROUPS) - 2)
-        finish(len(GROUPS) - 1)
+        cuts = [DIRECT, 512, 768, 896, S]
+        for e0, e1 in zip(cuts, cuts[1:]):
+            on_scalar(1, 3, e0, e1)
+        nc.scalar.copy(*pair(1, 1, cuts[-2], S))
+        for g in range(3):
+            place(1, 1, cuts[g], cuts[g + 1])
+            finish(g)
+        for g in range(3, len(GROUPS)):
+            finish(g)
         for g, n in enumerate(GROUPS):
             if g in VECTOR_GROUPS:
                 nc.vector.tensor_scalar_max(y[0][:, firsts[g] : firsts[g] + n], banks[g][:, :n], 0.0)
             else:
                 nc.scalar.activation(y[0][:, firsts[g] : firsts[g] + n], banks[g][:, :n], ACT.Relu)
-        wide = [psum.tile([P, HALF], F32, name="wide_%d" % h, tag="bank_%d" % (2 + h)) for h in range(2)]
+        wide = [psum.tile([P, HALF], F32, name="wide_%d" % h, tag="bank_%d" % (3 + h)) for h in range(2)]
         for h in range(2):
             for z in range(PASSES):
                 multiply(wide[h][:], 1, h * HALF, z, z == 0, z == 1)

from contextlib import ExitStack

import concourse.mybir as mybir

K, T, S, N, U = 1024, 2048, 1024, 256, 2048
FLOPS = 2 * K * S * N

F32 = mybir.dt.float32
BF16 = mybir.dt.bfloat16
I32 = mybir.dt.int32
U32 = mybir.dt.uint32
U16 = mybir.dt.uint16
U8 = mybir.dt.uint8
FP8X4 = mybir.dt.float8_e4m3fn_x4
FP4X4 = mybir.dt.float4_e2m1fn_x4
ACT = mybir.ActivationFunctionType
ADD = mybir.AluOpType.add

P = 128
PASSES = 2
BLOCKS = 2
HALF = 512
DIRECT = 256
ON_VECTOR = [[512, 640, 256, 576], [0, 448, 128]]
GROUPS = [256, 256, 128, 128, 128, 128]
VECTOR_GROUPS = (2, 4)
STORES = [
    (0, 576, 0), (0, 0, 384), (0, 640, 0), (0, 0, 448),
    (1, 448, 0), (1, 0, 416), (1, 256, 0), (1, 0, 384), (1, 192, 0), (1, 0, 224), (1, 0, 128),
]


def tile_picked_unmerge_relu_e_kernel(tc, xT, w1_words, w1_scales, res, offs, own, out):
    nc = tc.nc
    with ExitStack() as ctx:
        keep = ctx.enter_context(tc.tile_pool(name="keep", bufs=1))
        psum = ctx.enter_context(tc.psum_pool(name="psum", bufs=1))

        offs_sb = keep.tile([P, S // 16], U16, name="offs_sb")
        own_sb = keep.tile([P, U // 16], U16, name="own_sb")
        w_words = keep.tile([P, PASSES, 2 * N], U8, name="w_words", align_bytes=64)
        w_scales = keep.tile([P, PASSES, N], U8, name="w_scales", align_bytes=64)
        nc.vector.memset(w_scales[:].bitcast(I32), 0)

        x_rows = xT.rearrange("(z p j) t -> z j p t", z=PASSES, p=P, j=4)
        rows = [[keep.tile([P, T], F32, name="row_%d_%d" % (z, j)) for j in range(4)] for z in range(PASSES)]
        for z in range(PASSES):
            for j in range(4):
                nc.sync.dma_start(rows[z][j][:], x_rows[z, j])
                if z == 0 and j == 0:
                    nc.sync.dma_start(offs_sb[:], offs)
        for quad in range(4):
            nc.sync.dma_start(
                w_scales[32 * quad : 32 * quad + 4, :, :].bitcast(I32),
                w1_scales[:, 4 * quad : 4 * quad + 4, :].rearrange("z r c -> r z c").bitcast(I32),
            )
        nc.sync.dma_start(w_words[:].bitcast(I32), w1_words.rearrange("z p c -> p z c").bitcast(I32))
        nc.sync.dma_start(own_sb[:], own)
        res_sb = [keep.tile([P, U], F32, name="res_%d" % b) for b in range(BLOCKS)]
        for b in range(BLOCKS):
            nc.sync.dma_start(res_sb[b][:], res[b * P : (b + 1) * P, :])

        planes = [[keep.tile([P, 2, S], BF16, name="planes_%d_%d" % (z, u)) for u in range(2)] for z in range(PASSES)]
        woven = [keep.tile([P, S, 4], BF16, name="woven_%d" % z, align_bytes=64) for z in range(PASSES)]
        codes = [keep.tile([P, S], U32, name="codes_%d" % z, align_bytes=64) for z in range(PASSES)]
        scales = [keep.tile([P, S], U8, name="scales_%d" % z, align_bytes=64) for z in range(PASSES)]

        def picked(z, j, e0, e1):
            return rows[z][j][:].indirect(offs_sb[:, e0 // 16 : e1 // 16])

        def on_scalar(z, j, e0, e1):
            nc.scalar.activation(planes[z][j // 2][:, j % 2, e0:e1], picked(z, j, e0, e1), ACT.Copy)

        def on_vector(z, j, e0, e1):
            nc.vector.tensor_copy(planes[z][j // 2][:, j % 2, e0:e1], picked(z, j, e0, e1))

        def shared(z, j, e0):
            cut = S - ON_VECTOR[z][j]
            on_scalar(z, j, e0, cut)
            if cut < S:
                on_vector(z, j, cut, S)
            return cut

        def pair(z, u, e0, e1):
            return woven[z][:, e0:e1, 2 * u : 2 * u + 2], planes[z][u][:, :, e0:e1].rearrange("p j e -> p e j")

        def place(z, u, e0, e1):
            nc.vector.tensor_copy(*pair(z, u, e0, e1))

        def direct(j):
            nc.vector.tensor_copy(woven[1][:, :DIRECT, j], picked(1, j, 0, DIRECT))

        def quantize(z, e0, n):
            nc.vector.quantize_mx(
                out=codes[z][:, e0 : e0 + n].bitcast(FP8X4),
                scales=scales[z][:, e0 : e0 + n],
                in_=woven[z][:, e0 : e0 + n, :].rearrange("p e j -> p (e j)"),
            )

        def multiply(sums, b, e0, z, start, stop):
            n = sums.shape[1]
            nc.tensor.matmul_mx(
                out=sums,
                lhsT=w_words[:, z, 2 * P * b : 2 * P * (b + 1)].bitcast(FP4X4),
                lhsT_scale=w_scales[:, z, P * b : P * (b + 1)],
                rhs=codes[z][:, e0 : e0 + n].bitcast(FP8X4),
                rhs_scale=scales[z][:, e0 : e0 + n],
                start=start,
                stop=stop,
            )

        for u in range(2):
            shared(0, 2 * u, 0)
            shared(0, 2 * u + 1, 0)
            for h in range(2):
                place(0, u, h * HALF, (h + 1) * HALF)
        for h in range(2):
            quantize(0, h * HALF, HALF)

        shared(1, 0, 0)
        cut = shared(1, 1, 0)
        place(1, 0, cut, S)
        place(1, 0, 0, cut)
        shared(1, 2, DIRECT)
        direct(2)

        banks = [psum.tile([P, HALF], F32, name="bank_%d" % g, tag="bank_%d" % g) for g in range(len(GROUPS))]
        y = [keep.tile([P, S], F32, name="y_%d" % b) for b in range(BLOCKS)]
        firsts = [sum(GROUPS[:g]) for g in range(len(GROUPS))]
        for g, n in enumerate(GROUPS):
            multiply(banks[g][:, :n], 0, firsts[g], 0, True, False)

        def finish(g):
            quantize(1, firsts[g], GROUPS[g])
            multiply(banks[g][:, : GROUPS[g]], 0, firsts[g], 1, False, True)

        direct(3)
        cuts = [DIRECT, 512, 768, 896, S]
        for e0, e1 in zip(cuts, cuts[1:]):
            on_scalar(1, 3, e0, e1)
        nc.scalar.copy(*pair(1, 1, cuts[-2], S))
        for g in range(3):
            place(1, 1, cuts[g], cuts[g + 1])
            finish(g)
        for g in range(3, len(GROUPS)):
            finish(g)
        for g, n in enumerate(GROUPS):
            if g in VECTOR_GROUPS:
                nc.vector.tensor_scalar_max(y[0][:, firsts[g] : firsts[g] + n], banks[g][:, :n], 0.0)
            else:
                nc.scalar.activation(y[0][:, firsts[g] : firsts[g] + n], banks[g][:, :n], ACT.Relu)
        wide = [psum.tile([P, HALF], F32, name="wide_%d" % h, tag="bank_%d" % (3 + h)) for h in range(2)]
        for h in range(2):
            for z in range(PASSES):
                multiply(wide[h][:], 1, h * HALF, z, z == 0, z == 1)

        def owners(r0, r1):
            return own_sb[:, r0 // 16 : r1 // 16]

        done = [0] * BLOCKS
        for i, (b, fused, apart) in enumerate(STORES):
            if b == 1 and done[1] == 0:
                for h in range(2):
                    nc.scalar.activation(y[1][:, h * HALF : (h + 1) * HALF], wide[h][:], ACT.Relu)
            r0 = done[b]
            r1 = r0 + fused
            r2 = r1 + apart
            summed = keep.tile([P, r2 - r0], F32, name="summed_%d" % i)
            if fused:
                nc.vector.tensor_tensor(summed[:, :fused], y[b][:].indirect(owners(r0, r1)), res_sb[b][:, r0:r1], ADD)
            if apart:
                fetched = keep.tile([P, apart], F32, name="fetched_%d" % i)
                nc.scalar.activation(fetched[:], y[b][:].indirect(owners(r1, r2)), ACT.Copy)
                nc.vector.tensor_tensor(summed[:, fused:], fetched[:], res_sb[b][:, r1:r2], ADD)
            nc.sync.dma_start(out[b * P : (b + 1) * P, r0:r2], summed[:])
            done[b] = r2
